import numpy as np, ml_dtypes
CORES = [83,85,87,115,117,119]
N = 6
BF = ml_dtypes.bfloat16
def gentries(a):
    return np.ascontiguousarray(a.reshape(8, 16, -1).transpose(0, 2, 1)).reshape(8, -1)
def gtable(e):
    e = np.asarray(e); return np.ascontiguousarray(e.reshape(8, -1, 16).transpose(0, 2, 1)).reshape(128, -1).astype(np.int32)
W, S, ST, HOP = 4096, 192, 3, 5
def sig(v):
    return np.minimum(np.floor(v), 32640).astype(np.float32).astype(BF)
def parts(rng):
    sc = np.exp2(rng.integers(9, 16, (N, 8, 16, 1)).astype(np.float64))
    x = rng.random((N, 8, 16, W)) * sc
    t = np.floor(np.add.reduce(sc, axis=2)[:, :, None, :] * (0.15 + 0.2 * rng.random((N, 8, 16, 1))))
    o = np.argsort(rng.random((N, 8, S)), axis=-1)
    b = np.take_along_axis(o, np.floor(S * rng.random((N, 8, W)) ** 2).astype(np.int64), 2)
    nbr = rng.integers(0, W, (N, 8, 16, W)); L = rng.integers(0, W, (N, 8, S, 16))
    return x, t, b, nbr, L
def plant(rng, b, L):
    n = S // 8
    for q in range(N):
        for g in range(8):
            o = rng.permutation(S); pos = rng.permutation(W)[:3 * n].reshape(n, 3); b[q, g, pos] = o[:n, None]
            rows = np.argsort(rng.random((n, 16)), axis=1)[:, :6]
            L[q, g, o[:n, None], rows] = np.take_along_axis(pos, rng.integers(0, 3, (n, 6)), 1)
            rows = np.argsort(rng.random((n, 16)), axis=1)[:, :6]
            L[q, g, o[n:2 * n, None], rows] = np.take_along_axis(pos[rng.integers(0, n, n)], rng.integers(0, 3, (n, 6)), 1)
            L[q, g, o[2 * n]] = L[q, g, o[2 * n + 1]]; L[q, g, o[2 * n + 2]] = L[q, g, o[2 * n + 3]]
def pack(x, t, b, nbr, L):
    return {"tr": np.stack([gtable(a.reshape(8, -1)) for a in L]), "xs": np.ascontiguousarray(sig(x).reshape(N, 128, W)), "nb": np.ascontiguousarray(nbr.reshape(N, 128, W)).astype(np.int32),
            "lb": np.ascontiguousarray(b).astype(np.int32), "th": np.ascontiguousarray(t.reshape(N, 128, 1)).astype(np.int32)}
def setup_inputs(rng):
    x, t, b, nbr, L = parts(rng); plant(rng, b, L)
    return pack(x, t, b, nbr, L)
def setup_inputs_ties(rng):
    x, t, b, nbr, L = parts(rng)
    unit = rng.choice(np.array([1, 2, 64, 4096]), (N, 8, 1, 1)); unit[:, ::2] = 1
    x = unit * rng.integers(0, 3, (N, 8, 16, W)); x[:, 3] = 0
    t = unit * rng.integers(9, 17, (N, 8, 16, 1))
    b = rng.choice(np.array([0, 1, S // 2, S - 1]), (N, 8, W)); b[:, 1] = rng.integers(0, 24, (N, W)); b[:, 4] = rng.integers(S - 9, S, (N, W))
    return pack(x, t, b, nbr, L)
def setup_inputs_alike(rng):
    x, t, b, nbr, L = parts(rng)
    L[:, 0] = L[:, 0, :1].copy(); L[:, 1] = L[:, 1, :, :1].copy()
    b[:, 2] = 0; b[:, 3] = S - 1
    L[:, 4] = rng.choice(np.array([0, W - 1]), (N, S, 16)); nbr[:, 4] = rng.choice(np.array([0, W - 1, W // 2, 1]), (N, 16, W))
    L[:, 5] = rng.integers(W - 20, W, (N, S, 16))
    for g in (6, 7): L[:, g] = np.arange(S)[None, :, None] + S * rng.integers(0, W // S, (N, S, 16))
    b[:, 6] = np.arange(W) % S; b[:, 7] = (np.arange(W) % S + 1) % S
    return pack(x, t, b, nbr, L)
def setup_inputs_bounds(rng):
    x, t, b, nbr, L = parts(rng); plant(rng, b, L)
    t = np.where(rng.random((N, 8, 16, 1)) < 0.5, rng.choice(np.array([0, 524287]), (N, 8, 16, 1)), t); t[0] = 0; t[1] = 524287
    share = rng.choice(np.array([0.06, 0.3, 0.5, 0.94]), (N, 4, 1, 1))
    x[:, ::2] = np.where(rng.random((N, 4, 16, W)) < share, 32640, 0)
    return pack(x, t, b, nbr, L)
def setup_inputs_far(rng):
    x, t, b, nbr, L = parts(rng); plant(rng, b, L); i = np.arange(S); v = np.arange(W); m = W // S - 1
    low = rng.integers(0, 16, (N, 8, 16, W))
    for g, share in ((0, 0.5), (6, 0.4)):
        x[:, g] = np.where(rng.random((N, 16, W)) < share, 32640, low[:, g]); t[:, g] = rng.integers(200000, 320000, (N, 16, 1))
    for g, n in ((1, 1), (7, 2)):
        x[:, g] = np.where(np.argsort(rng.random((N, 16, W)), axis=1) < n, low[:, g], 32640); t[:, g] = rng.integers(0, 2 ** 17, (N, 16, 1))
    for g in (2, 4, 5):
        L[:, g] = i[None, :, None] + S * rng.integers(0, m, (N, S, 16)); b[:, g] = (v % S + 1) % S
    x[:, 2] = np.where(v < m * S, low[:, 2], 32640)
    np.put_along_axis(L[:, 2], rng.integers(0, 16, (N, S, 1)), i[None, :, None] + m * S, 2)
    t[:, 2] = np.where(rng.random((N, 16, 1)) < 0.5, rng.integers(0, 3, (N, 16, 1)), rng.integers(0, 522241, (N, 16, 1)))
    t[:, 2, 0::4] = rng.integers(393216, 489000, (N, 4, 1)); t[:, 2, 2::4] = rng.integers(327680, 393216, (N, 4, 1))
    t[:, 3] = rng.integers(0, 3, (N, 16, 1)); t[:, 3, ::2] = 0
    a = np.argsort(rng.random((N, W)), axis=1)[:, :S // 2]; L[:, 3, :S // 2] = a[:, :, None]
    np.put_along_axis(b[:, 3], a, (S // 2 + i[:S // 2])[None, :], 1)
    t[:, 4] = rng.integers(0, 3, (N, 16, 1))
    x[:, 5] = np.where(v < m * S, np.where(rng.random((N, 16, W)) < 0.5, 32640, low[:, 5]), rng.integers(15000, 17500, (N, 16, W)))
    nbr[:, 5] = rng.integers(m * S, W, (N, 16, W)); t[:, 5] = rng.integers(489600, 524288, (N, 16, 1))
    return pack(x, t, b, nbr, L)
def setup_inputs_spread(rng):
    x, t, b, nbr, L = parts(rng)
    x = rng.random((N, 8, 16, W)) * np.exp2(15 * rng.random((N, 8, 1, W))) * (rng.random((N, 8, 1, W)) > 0.0625)
    t = np.minimum(np.floor(np.exp2(10 + 9 * rng.random((N, 8, 16, 1)))), 524287)
    b = np.minimum(np.floor(S * rng.random((N, 8, W)) ** 4).astype(np.int64), S - 1)
    L = np.minimum(np.floor(W * rng.random((N, 8, S, 16)) ** 2).astype(np.int64), W - 1)
    plant(rng, b, L)
    return pack(x, t, b, nbr, L)
def check_inputs(d):
    bad = []; v = np.asarray(d["xs"]).astype(np.float32)
    if not (np.all(v == np.floor(v)) and np.min(v) >= 0 and np.max(v) <= 32640): bad.append("whole numbers and range of xs")
    for k, hi in (("tr", W - 1), ("nb", W - 1), ("lb", S - 1), ("th", 524287)):
        if np.min(d[k]) < 0 or np.max(d[k]) > hi: bad.append("range of " + k)
    return bad
def pick(X, c):
    return np.take_along_axis(X, c.reshape(N, 8, 1, S * 16), 3).reshape(N, 8, 16, S, 16)
def reference(tr, xs, nb, lb, th):
    X = xs.astype(np.float32).astype(np.int64).reshape(N, 8, 16, W); near = nb.astype(np.int64).reshape(N, 8, 16, W)
    t = th.astype(np.int64).reshape(N, 8, 1, 16); b = lb.astype(np.int64); i = np.arange(S)
    L = np.stack([gentries(a) for a in tr]).astype(np.int64).reshape(N, 8, S, 16)
    for st in range(ST):
        x = pick(X, L); y = np.add.reduce(x, axis=4) >> 4
        E = np.add.reduce(np.abs(x - y[..., None]), axis=2)
        p = np.take_along_axis(L, np.argmin(E, axis=3)[..., None], 3)[..., 0]
        v = np.take_along_axis(b, L.reshape(N, 8, S * 16), 2).reshape(N, 8, S, 16)
        votes = np.add.reduce((v[..., :, None] == v[..., None, :]).astype(np.int64), axis=4)
        H = np.take_along_axis(v, np.argmax(votes, axis=3)[..., None], 3)[..., 0]
        child = (H[..., :, None] == i) & (i[:, None] != i)
        don = np.min(np.where(child, i[:, None], S), axis=2); d0 = np.minimum(don, S - 1)[..., None]
        Ld = np.take_along_axis(L, d0, 2); Ed = np.take_along_axis(E, d0, 2)
        fill = np.take_along_axis(near, p[:, :, None, :], 3).swapaxes(2, 3)
        c = np.where((don < S)[..., None] & (Ed > t), Ld, fill)
        F = np.add.reduce(np.abs(pick(X, c) - y[..., None]), axis=2)
        new = np.where(F < E, c, L)
        again = np.argmax(p[..., :, None] == p[..., None, :], axis=3) < i
        new = np.where(again[..., None], fill, new)
        bb = np.concatenate([b, np.zeros((N, 8, 1), np.int64)], axis=2)
        np.put_along_axis(bb, np.where(again, W, p), np.broadcast_to(i, (N, 8, S)), 2); b = bb[..., :W]
        L = np.roll(new, HOP, axis=0) if st < ST - 1 else new
    return {"yl": np.stack([gtable(a.reshape(8, -1)) for a in L]).astype(np.float32), "yb": np.ascontiguousarray(b).astype(np.float32)}

@@ -1,0 +1,660 @@
+from concourse.mybir import AluOpType as AL, ActivationFunctionType as AF
+
+W, S, ST, HOP = 4096, 192, 3, 5
+HS, HO = (128, 64), (0, 128)
+R = 2
+NS = 16 // R
+SUB = 4
+P = dict(PEF=0.55, GF=1.55, OV=20, XL=130, SL=70, SEND=3000, EQA=(1, 2), LOOK=60,
+         BIAS={'C0': 46300, 'F0': 8000, 'T0': 48100, 'G': 9000, 'D': 47300, 'L': 11700, 'X0': 13700, 'E0': 19300,
+               'M0': 10700, 'V0': 9700, 'W0': 24400, 'V1': 8900, 'W1': 25000, 'H': 55300, 'K': -1100, 'F1': -700,
+               'T1': 40600, 'X1': 10800, 'C1': -8700, 'E1': 30000, 'P0': 2600, 'P1': -4000, 'M1': 8400, 'U1': -4500,
+               'U0': -2000, 'Y0': 7100, 'Y1': 6700},
+         DG=[[2, 9, 0, 5, 1, 8], [3, 1, 9, 2, 1, 0], [3, 8, 0, 7, 4, 0]],
+         FINE={'W0pv': 500, 'C1cx': 6500, 'Huw': -5000, 'C0cx': 500, 'P0ms': 5000, 'M0me': -7000, 'P0tl': 2000,
+               'T0pa': 5500, 'P1zc': 2000, 'E1py': 9500, 'T1nw': -1500, 'W0ab': -5000, 'Dai': -2000, 'T0su': -4000,
+               'P0ks': -5000, 'Gag': -7000, 'V1pv': 5500, 'Gsg': -5000, 'V0pv': 500, 'T0': -5000, 'P1tt': -2000,
+               'Hof': 7000, 'Y1lf': -3000, 'U1un': -4000, 'Y0lf': 2000, 'Dun': 500, 'Ht1': 500, 'Hsc': -500,
+               'T1mk': 4000, 'X0lu': 5000, 'Ddv': -1500, 'F0pa': -3000, 'P1ks': 3500, 'W0vs': 2000, 'C0au': 500,
+               'F1pa': 2500, 'Hpv': 2000, 'W1hj': 4500, 'W0hc': 500, 'X1lu': 500, 'C1aa': 1500, 'W1hi': -8000,
+               'T1': -10000, 'W1ev': 1500, 'P1tl': 2000, 'W1hs': 7500, 'D': 500, 'W0mh': 2000, 'Heq': 5000,
+               'P0pg': 1500, 'W0hr': -5000, 'W0hs': -5000, 'W1mh': -7500, 'Ht2': 2000, 'U0un': -5500, 'T1su': -1000,
+               'Gpg': 4000, 'W0hj': -2000, 'W0ev': -1500, 'W0pd': 500, 'C1au': 2000, 'Y0l4': -2500, 'E0pa': -2000,
+               'X0x0': 500, 'Daj': -5000, 'P1pu': -500, 'T0mk': 1000, 'T0nw': 2000, 'P0tt': -500})
+MAGIC = 12582912.0
+F, B, I, U = "float32", "bfloat16", "int32", "uint16"
+
+SCRATCH = {}
+BUF = {}
+POOLED = ("pci pki pgi p1i p2i sa sa2 sbi sb2 jgi c15i czi saf sbf rw i32f j192 j4096 half zero wrow wtmp wsc thr thd seg0 "
+          "rst idf bof bom ib i16 bob kc kh i192 ibig ones qg qk im16 wbig diag cy nthd nthr pick pik2 pik5 kcc kci prf "
+          "prb par q2 q8 ibc").split()
+
+
+def _sb(name, n, dt, where="sbuf"):
+    if name in POOLED:
+        pool = "pool_" + dt
+        at = SCRATCH[pool][1][1] if pool in SCRATCH else 0
+        SCRATCH[pool] = ("sbuf", [128, at + (n + 15) // 16 * 16], dt)
+        BUF[name] = (where, [128, n], dt, pool, at)
+    else:
+        SCRATCH[name] = (where, [128, n], dt)
+        BUF[name] = (where, [128, n], dt, name, 0)
+
+
+for _n, _w, _d in [
+    ("xw", 2 * W, B), ("nbw", W, I), ("lw", W + S, B), ("tri", S, I), ("lbi", 256, I), ("lbb", 256, B), ("thi", 4, I),
+    ("jrow", S, B), ("pci", 4, I), ("pki", 4, I), ("pgi", 4, I), ("p1i", 4, I), ("p2i", 4, I), ("cols", 24, F),
+    ("qg", 128, B), ("qk", S, B), ("q2", 128, B), ("q8", 64, B), ("kci", 64, B), ("kcc", 64, B), ("prf", 64, F),
+    ("prb", 64, B), ("par", 128, B), ("ibc", 64, B), ("czi", 8, I), ("cz", 8, U),
+    ("ib", 128, B), ("idf", 128, F), ("bob", 128, B), ("bof", 128, F), ("bom", 128, F), ("i32f", 8, F), ("im16", 8, B),
+    ("wbig", 144, B), ("pm_s", 1024, B), ("dm_s", 1024, B), ("rm_s", 1024, B), ("sa", 8, I), ("sa2", 8, I), ("saf", 8, F),
+    ("sbi", 8, I), ("sb2", 8, I), ("sbf", 8, F), ("rw", 8, F), ("kc", 128, B), ("kh", 128, B), ("i192", 128, B),
+    ("ibig", 128, B), ("ones", 128, B), ("diag", S, B), ("seg0", S, F), ("rst", 128, F), ("jgi", 12, I),
+    ("j192", 12, F), ("j4096", 12, F), ("half", S, F), ("zero", S, F), ("wrow", S, F), ("thr", S, F), ("thd", S, F),
+    ("wtmp", S, F), ("wsc", S, F), ("c15i", 8, I), ("c15", 8, U), ("i16", 128, B), ("cy", 128, B), ("nthd", S, B),
+    ("nthr", S, B), ("sg", S, B), ("pick", S, F), ("pik2", S, F), ("pik5", S, F),
+    ("lf0", S, F), ("lf1", S, F), ("l4", S, F), ("unb", S, F), ("uw", 2 * S, F), ("pu", S, U), ("pgs", S, F),
+    ("pgu", 12, U), ("pgf", 12, F), ("hi", S, I), ("hj", S, I), ("hrs", S, B), ("hsc", S, F), ("hc", 12, F),
+    ("hp", 12, F), ("eqh", 1248, B), ("eqp", 1248, B), ("sc", S, F), ("t0", 12, F), ("t1", 12, F), ("t2", 12, F),
+    ("offu", 12, U), ("ag", S, B), ("agd", 128, B), ("scp", S, F), ("t3", 12, F), ("t4", 12, F), ("t5", 12, F),
+    ("ofp", 12, U), ("un", S, F), ("ai", S, I), ("aj", S, I), ("dv", S, F), ("ksc", 64, F), ("zc", 128, F),
+    ("mkc", 64, B),
+]:
+    _sb(_n, _w, _d)
+for _c in range(2):
+    _h = HS[_c]
+    for _n, _w, _d in [("x", 16 * _h, B), ("cx", 16 * _h, B), ("v", 16 * _h, B), ("me", 16 * _h, F), ("mf", 16 * _h, F),
+                       ("ys", _h, F), ("ac", 4 * _h, B), ("ks", 128, F), ("ms", 128, F), ("tt", 128, B), ("tl", _h, F),
+                       ("ab", 4 * _h, B), ("vs", _h, B), ("ev", 9 * _h, B), ("mh", 128, F), ("zz", 128, F),
+                       ("aa", _h, F), ("au", _h, U), ("mk", 128, B), ("nw", _h, F)]:
+        _sb("%s%d" % (_n, _c), _w, _d)
+    for _t in range(ST):
+        _sb("lu%d%d" % (_t, _c), _h, U)
+    for _t in range(ST - 1):
+        _sb("su%d%d" % (_t, _c), _h, U)
+for _n in ("py0", "py1", "pa0", "pa1", "pv0", "pv1", "pd0", "pd1"):
+    _sb(_n, 512, F, "psum")
+
+DMAS = ["d_tr", "d_lb", "d_th", "d_xs", "d_lw", "d_nb", "d_x2", "d_y0", "d_y1", "d_yb"]
+ARRS = ["arr%d%d" % (t, c) for t in range(1, ST) for c in range(2)]
+SEMAPHORES = ["s_dve", "s_act", "s_pe", "s_pool", "sent"] + DMAS + ARRS
+
+
+def A(name, c0=0, c1=None, st=1, p=128):
+    return (name, p, c0, BUF[name][1][1] if c1 is None else c1, st)
+
+
+def IND(win, off):
+    return ("#", win, off)
+
+
+def _n(a):
+    return 16 * _n(a[2]) if a[0] == "#" else len(range(a[2], a[3], a[4]))
+
+
+def _ap(T, a):
+    if not isinstance(a, tuple):
+        return a
+    if a[0] == "#":
+        return _ap(T, a[1]).indirect(_ap(T, a[2]))
+    buf, at = BUF[a[0]][3:]
+    if a[4] == 1:
+        return T[buf][0:a[1], at + a[2]:at + a[3]]
+    return T[buf][0:a[1], at + a[2]:at + a[3]:a[4]]
+
+
+def _ps(a):
+    return a[0] != "#" and BUF[a[0]][0] == "psum"
+
+
+def _two(a):
+    return BUF[a[0]][2] in (B, U)
+
+
+def build():
+    ops = []
+    OV, DG = P["OV"], P["DG"]
+    tag = ["K"]
+
+    def add(eng, kind, args, outs, ins, cost, **kw):
+        rd, wr = [], []
+        for a in ins:
+            if isinstance(a, tuple):
+                rd += [a[1], a[2]] if a[0] == "#" else [a]
+        for a in outs:
+            if a[0] == "#":
+                wr.append(a[1])
+                rd.append(a[2])
+            else:
+                wr.append(a)
+        o = dict(tag=tag[0], eng=eng, kind=kind, args=args, rd=rd, wr=wr, cost=cost, extra=[], lat=0)
+        o["fine"] = tag[0] + (wr[0][0][:2] if wr else "")
+        o.update(kw)
+        ops.append(o)
+        return o
+
+    def vcost(out, ins, base):
+        n = _n(out)
+        if out[0] == "#":
+            return 70 + 3.5 * n
+        if ins[0][0] == "#":
+            return 70 + P["GF"] * n
+        return OV + max(64, base * n)
+
+    def cp(out, a, eng="dve"):
+        half = eng == "dve" and out[0] != "#" and a[0] != "#" and _two(out) and _two(a)
+        return add(eng, "cp", (out, a), [out], [a], vcost(out, [a], 0.5 if half else 1))
+
+    def ts(out, a, s1, s2, o0, o1=None):
+        return add("dve", "ts", (out, a, s1, s2, o0, o1), [out], [a, s1, s2],
+                   vcost(out, [a], 0.5 if _two(out) and _two(a) else 1))
+
+    def tt(out, a, b, op):
+        return add("dve", "tt", (out, a, b, op), [out], [a, b], vcost(out, [a], 1 if _ps(a) or _ps(b) else 2))
+
+    def scan(out, d0, d1, init, o0, o1):
+        return add("dve", "scan", (out, d0, d1, init, o0, o1), [out], [d0, d1], vcost(out, [d0], 1))
+
+    def ms(out, val):
+        return add("dve", "ms", (out, val), [out], [], OV + max(64, _n(out) * (0.5 if _two(out) else 1)))
+
+    def act(out, a, fn, bias, scale=1.0):
+        return add("act", "act", (out, a, fn, bias, scale), [out], [a, bias], vcost(out, [a], 1))
+
+    def mm(out, l, r, st, sp):
+        c = max(min(64, _n(l)), _n(r)) * (4 if BUF[l[0]][2] == F else 1) * P["PEF"] + 4
+        return add("pe", "mm", (out, l, r, st, sp), [out], [l, r], c)
+
+    def iota(out, pat, base, cm):
+        return add("pool", "iota", (out, pat, base, cm), [out], [], 160 + 2 * _n(out))
+
+    def dma(q, sem, fn, outs, ins, lat):
+        return add(q, "dma", fn, outs, ins, 60, sem=sem, lat=lat)
+
+    col = lambda j, p=128: A("cols", j, j + 1, 1, p)
+    PF, PK, PG, P16, M0, KM, KH, TH, G16, C1, C4096, PK4, PK2, PK5, PK6, P1, PH, KP, MB, P7 = range(20)
+
+    ms(A("lw"), 0.0)
+    ld = [dma("sp", "d_tr", lambda T: (T.tri[:, :], T.tr[:, :]), [A("tri")], [], 2400),
+          dma("sp", "d_lb", lambda T: (T.lbi[:, :], T.lb[:, :]), [A("lbi")], [], 2400),
+          dma("sp", "d_xs", lambda T: (T.xw[:, 0:W], T.xs[:, :]), [A("xw", 0, W)], [], 6500),
+          dma("sp", "d_th", lambda T: (T.thi[:, 0:1], T.th[:, :]), [A("thi", 0, 1)], [], 6500)]
+    cp(A("lbb"), A("lbi"))
+    ld += [dma("sp", "d_lw", lambda T: (T.lw[0:128:16, 0:W], T.lbb[:, :]), [A("lw", 0, W)], [A("lbb")], 4000),
+           dma("sp", "d_nb", lambda T: (T.nbw[:, :], T.nb[:, :]), [A("nbw")], [], 9000),
+           dma("sp", "d_x2", lambda T: (T.xw[:, W:2 * W], T.xs[:, :]), [A("xw", W, 2 * W)], [], 12000)]
+    for a, b in zip(ld, ld[1:]):
+        b["after"] = a
+
+    iota(A("pci", 0, 1), [[0, 1]], 0, 1)
+    iota(A("jrow"), [[1, S]], 0, 0)
+    iota(A("qg"), [[1, 8], [0, 16]], 0, 0)
+    iota(A("qk"), [[0, 12], [1, 16]], 0, 0)
+    iota(A("c15i"), [[16, 8]], 15, 0)
+    iota(A("sa"), [[-1, 8]], 15, 1)
+    iota(A("sbi"), [[1, 8]], 1, 1)
+    iota(A("jgi"), [[16, 12]], 0, 0)
+    pc, pk = A("pci", 0, 1), A("pki", 0, 1)
+    ts(pk, pc, 15, None, AL.bitwise_and)
+    ts(A("pgi", 0, 1), pc, 4, None, AL.arith_shift_right)
+    cp(col(PF), pc)
+    cp(col(PK), pk)
+    cp(col(PG), A("pgi", 0, 1))
+    ts(col(P16), pc, 16.0, None, AL.add)
+    ts(col(M0), pk, 0.0, None, AL.is_equal)
+    ts(col(KM), pk, -15.0, None, AL.add)
+    ts(col(KH), pk, -512.0, 7680.0, AL.mult, AL.add)
+    ts(col(TH), A("thi", 0, 1), -16.0, -0.5, AL.mult, AL.add)
+    ts(col(G16), A("pgi", 0, 1), 16.0, None, AL.mult)
+    ts(col(PK4), pk, 4096.0, -61440.0, AL.mult, AL.add)
+    ts(col(PK2), pk, 2.0, -30.0, AL.mult, AL.add)
+    ts(col(PK5), pk, 512.0, -7680.0, AL.mult, AL.add)
+    ts(col(PK6), pk, 512.0, -7488.0, AL.mult, AL.add)
+    ms(col(C1), 1.0)
+    ms(col(C4096), 4096.0)
+    j128 = A("jrow", 0, 128)
+    ts(A("ib"), j128, col(PF), None, AL.is_equal)
+    ts(A("i16"), j128, col(PF), 0.0625, AL.is_equal, AL.mult)
+    ms(A("cy"), -0.46875)
+    ts(A("idf"), j128, col(PF), None, AL.is_equal)
+    ts(A("kc"), j128, col(PF), col(KM), AL.is_equal, AL.mult)
+    ts(A("kh"), j128, col(PF), col(KH), AL.is_equal, AL.mult)
+    ts(A("i192"), j128, col(PF), 192.0, AL.is_equal, AL.mult)
+    ts(A("ibig"), j128, col(PF), -float(2 ** 26), AL.is_equal, AL.mult)
+    ts(A("bob"), A("qg"), col(PG), None, AL.is_equal)
+    ts(A("bof"), A("qg"), col(PG), None, AL.is_equal)
+    ts(A("bom"), A("qg"), col(PG), -16.0, AL.is_equal, AL.mult)
+    ts(A("i32f"), A("jrow", 0, 8), col(PG), 32.0, AL.is_equal, AL.mult)
+    ts(A("im16"), A("jrow", 0, 8), col(PG), -16.0, AL.is_equal, AL.mult)
+    ts(A("wbig"), A("jrow", 0, 144), col(P16), col(M0), AL.is_equal, AL.mult)
+    ts(A("sa2"), A("sa"), 15, None, AL.bitwise_and)
+    ts(A("saf"), A("sa2"), col(G16), None, AL.add)
+    ts(A("sb2"), A("sbi"), 15, None, AL.bitwise_and)
+    ts(A("sbf"), A("sb2"), col(PK), col(G16), AL.min, AL.add)
+    ms(A("rw", 0, 7), 8192.0)
+    ts(A("rw", 7, 8), pk, 8.0, 8192.0, AL.is_lt, AL.mult)
+    for s in range(8):
+        ts(A("pm_s", 128 * s, 128 * s + 128), j128, A("saf", s, s + 1), -1.0, AL.is_equal, AL.mult)
+        d = A("pd%d" % (s // 4), 128 * (s % 4), 128 * (s % 4 + 1))
+        mm(d, A("ib"), A("ib"), True, False)
+        mm(d, A("ib"), A("pm_s", 128 * s, 128 * s + 128), False, True)
+        ts(A("rm_s", 128 * s, 128 * s + 128), j128, A("sbf", s, s + 1), A("rw", s, s + 1), AL.is_equal, AL.mult)
+    for s in range(2):
+        cp(A("dm_s", 512 * s, 512 * s + 512), A("pd%d" % s), "act")
+    ms(A("ones"), 1.0)
+    ts(A("diag"), A("qk"), col(PK), None, AL.is_equal)
+    for n, step in (("pick", 4096.0), ("pik2", 2.0), ("pik5", 512.0)):
+        ts(A(n), A("diag"), -float(2 ** 20), step, AL.mult, AL.add)
+    ts(A("seg0"), A("qk"), 0.0, None, AL.not_equal)
+    ts(A("rst"), A("qk", 0, 128), 0.0, float(2 ** 25), AL.is_equal, AL.mult)
+    ts(A("j192"), A("jgi"), col(PK), 192.0, AL.add, AL.add)
+    ts(A("j4096"), A("jgi"), col(PK), 4096.0, AL.add, AL.add)
+    ms(A("half"), 0.5)
+    ms(A("zero"), 0.0)
+    scan(A("wrow"), A("half"), A("zero"), float(2 ** 96), AL.mult, AL.add)
+    ts(A("thr"), A("wrow"), 2.5, None, AL.mult)
+    ts(A("wtmp"), A("qk"), col(PK), float(2 ** 98), AL.not_equal, AL.mult)
+    tt(A("thd"), A("wtmp"), A("thr"), AL.add)
+    ts(A("nthr"), A("wrow"), -2.5, None, AL.mult)
+    ts(A("nthd"), A("thd"), -1.0, None, AL.mult)
+    tt(A("wtmp"), A("wrow"), A("diag"), AL.mult)
+    scan(A("wsc"), A("seg0"), A("wtmp"), 0.0, AL.mult, AL.max)
+    cp(A("c15"), A("c15i"))
+    cp(A("uw", S, 2 * S), A("zero"), "act")
+    for n in ("ks1", "ms1", "mh1"):
+        cp(A(n), A("zero", 0, 128), "act")
+    iota(A("q2"), [[0, 8], [1, 2], [0, 8]], 0, 0)
+    iota(A("q8"), [[1, 8], [0, 8]], 0, 0)
+    iota(A("kci"), [[0, 8], [1, 8]], 0, 0)
+    iota(A("czi"), [[8, 8]], 0, 0)
+    ts(A("p1i", 0, 1), pc, 1, None, AL.bitwise_and)
+    ts(A("p1i", 1, 2), pc, 7, None, AL.bitwise_and)
+    ts(A("p2i", 0, 1), pc, 1, None, AL.arith_shift_right)
+    cp(col(P1), A("p1i", 0, 1))
+    cp(col(PH), A("p2i", 0, 1))
+    cp(col(P7), A("p1i", 1, 2))
+    ts(col(KP), A("p1i", 0, 1), 8.0, -15.0, AL.mult, AL.add)
+    ts(col(MB), pk, 0.0, -float(2 ** 26), AL.is_equal, AL.mult)
+    ts(A("kcc"), A("kci"), col(KP), None, AL.add)
+    ts(A("prf"), A("jrow", 0, 64), col(PH), None, AL.is_equal)
+    ts(A("prb"), A("jrow", 0, 64), col(PH), None, AL.is_equal)
+    ts(A("par"), A("q2"), col(P1), None, AL.is_equal)
+    ts(A("ibc"), A("q8"), col(PG), col(MB), AL.is_equal, AL.mult)
+    ts(A("cz"), A("czi"), col(P7), None, AL.add)
+
+    def gather(dst, win, off, t, j):
+        q = HS[j % 2] // SUB
+        for u in range(SUB):
+            o = cp(A(dst, 16 * q * u, 16 * q * (u + 1)), IND(win, A(off, q * u, q * (u + 1))),
+                   "dve" if DG[t][j] >> u & 1 else "act")
+            o["gat"] = (t, j, u)
+
+    def energy(c, x, m, last):
+        pa, py, h = "pa%d" % c, "py%d" % c, HS[c]
+        n = h * R
+        if c == 1:
+            mm(A(pa, 128, 192), A("ib"), A("kcc"), True, False)
+            for i in range(8):
+                mm(A(pa, 128 + i, 192, 8), A(x, i, None, 8), A("im16"), False, False)
+            for i in range(8):
+                tt(A(m, i * n, (i + 1) * n), A(x, i, None, 8), A(py, 0, n), AL.max)
+                mm(A(pa, 128 + i, 192, 8), A(m, i * n, (i + 1) * n), A("i32f"), False, last is None and i == 7)
+            if last is not None:
+                mm(A(pa, 128, 192), A("agd"), A("ibc"), False, True)
+            return
+        mm(A(pa, 128, 256, 1, h), A("ones", 0, h), A("kc"), True, False)
+        for k in range(16):
+            mm(A(pa, 128 + k, 256, 16, h), A(x, k, None, 16), A("im16"), False, False)
+        for i in range(NS):
+            tt(A(m, i * n, (i + 1) * n), A(x, i, None, NS), A(py, 0, n), AL.max)
+            for a in range(R):
+                end = last is None and i == NS - 1 and a == R - 1
+                mm(A(pa, 128 + NS * a + i, 256, 16, h), A(m, i * n + a, (i + 1) * n, R), A("i32f"), False, end)
+        if last is not None:
+            mm(A(pa, 128, 256, 1, h), last, A("ibig"), False, True)
+
+    def firsts(eq, row, scal, bank, less):
+        o = 0
+        mm(A(bank, 256, 448), A("ib"), A(less), True, False)
+        for hh in range(12):
+            n = S - 16 * hh
+            ts(A(eq, o, o + n), A(row, 16 * hh, S), A(scal, hh, hh + 1), A("wsc", 16 * hh + 15, 16 * hh + 16),
+               AL.is_equal, AL.mult)
+            mm(A(bank, 256 + 16 * hh, 448), A("bob"), A(eq, o, o + n), False, hh == 11)
+            o += n
+
+    H = lambda name, c: A(name, HO[c], HO[c] + HS[c])
+    G = lambda name, c: A(name, HO[c] // 16, (HO[c] + HS[c]) // 16)
+    E15 = lambda name, c: A(name, HO[c] + 15, HO[c] + HS[c], 16)
+    sends = {}
+    for t in range(ST):
+        lf = "lf%d" % (t % 2)
+        for c in range(2):
+            lu = "lu%d%d" % (t, c)
+            tag[0] = "X%d" % c
+            if t == 0:
+                cp(A(lu), H("tri", c))
+            else:
+                add(None, "recv", None, [A(lu)], [], 0, sem="arr%d%d" % (t, c), extra=[sends[t - 1, c]])
+            gather("x%d" % c, A("xw", 0, W), lu, t, c)
+            tag[0] = "Y%d" % c
+            cp(H(lf, c), A(lu))
+            act(H("l4", c), H(lf, c), AF.Identity, col(C4096))
+        cp(A("uw", 0, S), A("zero"), "act")
+        for c in range(2):
+            n = lambda s: "%s%d" % (s, c)
+            pa, py, h = n("pa"), n("py"), HS[c]
+            tag[0] = "E%d" % c
+            mm(A(pa, 0, h), A("ib"), A("cy", 0, h), True, False)
+            for k in range(16):
+                mm(A(pa, 0, h), A("i16"), A(n("x"), k, None, 16), False, k == 15)
+            for i in range(R):
+                ts(A(py, i, h * R, R), A(pa, 0, h), MAGIC, -MAGIC, AL.add, AL.add)
+            tag[0] = "M%d" % c
+            energy(c, n("x"), n("me"), None)
+            cp(A(n("ys")), A(py, 0, h * R, R), "act")
+            tag[0] = "P%d" % c
+            et = A(pa, 128, 256, 1, h)
+            kl, kr = A(n("ks"), p=h), A("idf", 0, h, 1, h)
+            if c == 1:
+                cp(A("ksc"), A(pa, 128, 192), "act")
+                tt(A("zc"), IND(A("ksc"), A("cz")), A("par"), AL.mult)
+                et = A(pa, 256, 384, 1, h)
+                mm(et, A("prf"), A("zc"), True, True)
+                kl, kr = A("zc"), A("prf")
+            scan(A(n("ms"), p=h), A("rst", p=h), et, 0.0, AL.add, AL.min)
+            cp(A(n("ks"), p=h), et, "act")
+            tt(A(n("tt")), IND(A(n("ms")), A("c15")), A(n("ks")), AL.is_equal)
+            mm(A(pa, 0, h), A(n("tt"), p=h), A("ib", 0, h, 1, h), True, True)
+            tag[0] = "U%d" % c
+            mm(A(py, 256, 256 + h), A("bom"), A(n("ys")), True, False)
+            mm(A(py, 256, 256 + h), kl, kr, False, True)
+            act(H("unb", c), A(py, 256, 256 + h), AF.Sign, col(TH))
+            tag[0] = "P%d" % c
+            tt(A(n("tl")), A(pa, 0, h), H(lf, c), AL.mult)
+            mm(A(pa, 0, h), A("bof"), A(n("tl")), True, True)
+            scan(H("pgs", c), A("pick", 0, h), A(pa, 0, h), 0.0, AL.add, AL.max)
+            cp(H("pu", c), A(pa, 0, h))
+            ts(G("pgu", c), E15("pgs", c), col(PK4), None, AL.add)
+        for c in range(2):
+            n = lambda s: "%s%d" % (s, c)
+            pv, h = n("pv"), HS[c]
+            tag[0] = "V%d" % c
+            gather(n("v"), A("lw", 0, W), "lu%d%d" % (t, c), t, 2 + c)
+            for k in range(16):
+                mm(A(pv, 0, h), A("wbig", 16 - k, 144 - k), A(n("v"), k, None, 16), k == 0, k == 15)
+            tag[0] = "W%d" % c
+            cp(A(n("vs")), A(pv, 0, h), "act")
+            tt(A(n("ev"), 8 * h, 9 * h), A(pv, 0, h), H("jrow", c), AL.is_equal)
+            for s in range(8):
+                mm(A("pd%d" % (s // 4), h * (s % 4), h * (s % 4 + 1)), A("dm_s", 128 * s, 128 * s + 128), A(n("vs")), True, True)
+            kt = A(pv, 128, 256, 1, h)
+            mm(kt, A("ones", 0, h), A("kh"), True, False)
+            mm(kt, A(n("vs")), A("ib"), False, False)
+            mm(kt, A(n("ev"), 8 * h, 9 * h), A("i192"), False, False)
+            for b, tmp in ((0, "ac"), (1, "ab")):
+                e, d = A(n("ev"), 4 * h * b, 4 * h * (b + 1)), A("pd%d" % b, 0, 4 * h)
+                if P["EQA"][c] > 1 - b:
+                    act(A(n(tmp)), d, AF.Abs, 0.0)
+                    act(e, A(n(tmp)), AF.Relu, col(C1), -1.0)
+                else:
+                    ts(e, d, 0.0, None, AL.is_equal)
+            for s in range(8):
+                mm(kt, A(n("ev"), h * s, h * s + h), A("rm_s", 128 * s, 128 * s + 128), False, s == 7)
+            scan(A(n("mh"), p=h), A("seg0", 0, 128, 1, h), kt, 0.0, AL.mult, AL.max)
+            cp(A(n("zz")), IND(A(n("mh")), A("c15")), "act")
+            mm(A(pv, 256, 256 + h), A(n("zz"), p=h), A("idf", 0, h, 1, h), True, True)
+            cp(H("hi", c), A(pv, 256, 256 + h))
+            ts(H("hj", c), H("hi", c), 511, None, AL.bitwise_and)
+            ts(H("hrs", c), H("hj", c), -192.0, None, AL.add)
+            scan(H("hsc", c), A("pik5", 0, h), H("hrs", c), 0.0, AL.add, AL.max)
+            ts(G("hc", c), E15("hsc", c), col(PK5), None, AL.add)
+        tag[0] = "H"
+        ts(A("hp"), A("hsc", 15, S, 16), col(PK6), None, AL.add)
+        firsts("eqh", "hrs", "hc", "pv0", "nthd")
+        scan(A("sc"), A("seg0"), A("pv0", 256, 448), 0.0, AL.mult, AL.max)
+        ts(A("t0"), A("sc", 15, S, 16), 0.0, 1024.0, AL.is_gt, AL.mult)
+        tt(A("t1"), A("t0"), A("j192"), AL.min)
+        tt(A("t2"), A("t1"), A("hp"), AL.max)
+        cp(A("offu"), A("t2"))
+        tt(IND(A("uw"), A("offu")), A("unb"), A("l4"), AL.mult)
+        for c in range(2):
+            tag[0] = "C%d" % c
+            tt(A("aa%d" % c), IND(A("nbw"), G("pgu", c)), H("uw", c), AL.max)
+            cp(A("au%d" % c), A("aa%d" % c))
+            gather("cx%d" % c, A("xw"), "au%d" % c, t, 4 + c)
+        tag[0] = "G"
+        ts(A("pgf"), A("pgs", 15, S, 16), col(PK4), None, AL.add)
+        firsts("eqp", "pu", "pgf", "pv1", "nthr")
+        act(A("sg"), A("pv1", 256, 448), AF.Sign, 0.0)
+        act(A("pd0", 0, S), A("sg"), AF.Relu, 0.0, -1.0)
+        act(A("ag"), A("sg"), AF.Relu, 0.0)
+        cp(A("pd0", S, 2 * S), A(lf), "act")
+        for a in range(2):
+            cp(A("agd", a, 128, 2), H("ag", 1), "act")
+        tag[0] = "L"
+        scan(A("scp"), A("pik2"), A("ag"), 0.0, AL.add, AL.max)
+        ts(A("t5"), A("scp", 15, S, 16), col(PK2), 8192.0, AL.add, AL.mult)
+        tt(A("t3"), A("t5"), A("j4096"), AL.min)
+        tt(A("t4"), A("t3"), A("pgf"), AL.max)
+        cp(A("ofp"), A("t4"))
+        cp(IND(A("lw"), A("ofp")), A("jrow"))
+        tag[0] = "D"
+        tt(A("un"), A("uw", 0, S), A("pd0", 0, S), AL.mult)
+        tt(A("ai"), IND(A("nbw"), A("pgu")), A("un"), AL.max)
+        ts(A("aj"), A("ai"), 4095, None, AL.bitwise_and)
+        tt(A("dv"), A("aj"), A("pd0", S, 2 * S), AL.subtract)
+        if t == ST - 1:
+            dma("pool", "d_yb", lambda T: (T.yb[:, :], T.lw[0:128:16, 0:W]), [], [A("lw", 0, W)], 4500)
+        for c in range(2):
+            n = lambda s: "%s%d" % (s, c)
+            pa, h = n("pa"), HS[c]
+            tag[0] = "F%d" % c
+            energy(c, n("cx"), n("mf"), H("ag", c))
+            tag[0] = "T%d" % c
+            if c == 1:
+                tt(A("mkc"), A(pa, 128, 192), A("ksc"), AL.is_lt)
+                tt(A(n("mk")), IND(A("mkc"), A("cz")), A("par"), AL.mult)
+                mm(A(pa, 0, h), A(n("mk")), A("prb"), True, True)
+            else:
+                tt(A(n("mk"), p=h), A(pa, 128, 256, 1, h), A(n("ks"), p=h), AL.is_lt)
+                mm(A(pa, 0, h), A(n("mk"), p=h), A("ib", 0, h, 1, h), True, True)
+            tt(A(pa, 256, 256 + h), A(pa, 0, h), H("dv", c), AL.mult)
+            tt(A(n("nw")), A(pa, 256, 256 + h), H(lf, c), AL.add)
+            if t < ST - 1:
+                su = "su%d%d" % (t, c)
+                cp(A(su), A(n("nw")))
+                sends[t, c] = add("pool", "send", (su, "lu%d%d" % (t + 1, c), "arr%d%d" % (t + 1, c)), [], [A(su)],
+                                  300, lat=P["SEND"])
+            else:
+                dma("sp", "d_y%d" % c,
+                    (lambda cc: lambda T: (T.yl[:, HO[cc]:HO[cc] + HS[cc]], T["nw%d" % cc][:, :]))(c), [], [A(n("nw"))], 2600)
+    return ops
+
+
+def _deps(ops):
+    hist, bank = {}, {}
+    for i, o in enumerate(ops):
+        o["i"] = i
+        hard, soft = set(), set()
+        for a, w in [(a, False) for a in o["rd"]] + [(a, True) for a in o["wr"]]:
+            cs = frozenset(range(a[2], a[3], a[4]))
+            keep = []
+            for (j, cj, wj) in hist.get(a[0], []):
+                hit = (w or wj) and j != i and not cs.isdisjoint(cj)
+                if hit:
+                    if o["kind"] == "mm" and ops[j]["kind"] == "mm":
+                        soft.add(j)
+                    else:
+                        hard.add(j)
+                if not (w and hit and cj <= cs and o["kind"] != "mm"):
+                    keep.append((j, cj, wj))
+            keep.append((i, cs, w))
+            hist[a[0]] = keep
+            if _ps(a):
+                e = o["eng"]
+                st = bank.setdefault(a[0], dict(e=e, cur=[], prev=[]))
+                if st["e"] != e:
+                    st["prev"], st["cur"], st["e"] = st["cur"], [], e
+                hard.update(st["prev"])
+                if e == "pe" and st["cur"]:
+                    soft.add(st["cur"][-1])
+                if i not in st["cur"]:
+                    st["cur"].append(i)
+        if "after" in o:
+            soft.add(o["after"]["i"])
+        o["hard"] = sorted(hard)
+        o["soft"] = sorted(soft - hard)
+        o["time"] = [x["i"] for x in o["extra"]]
+
+
+def schedule():
+    XL, SL, LOOK = P["XL"], P["SL"], P["LOOK"]
+    ops = build()
+    _deps(ops)
+    n = len(ops)
+    succ = [[] for _ in ops]
+    left = [0] * n
+    for o in ops:
+        d = set(o["hard"]) | set(o["soft"]) | set(o["time"])
+        left[o["i"]] = len(d)
+        for j in d:
+            succ[j].append(o["i"])
+    pr = [0.0] * n
+    for i in range(n - 1, -1, -1):
+        o = ops[i]
+        pr[i] = o["cost"] + max(
+            [pr[j] + (0 if i in ops[j]["soft"] else o["lat"] + (SL if o["eng"] == ops[j]["eng"] else XL)) for j in succ[i]]
+            + [o["lat"]])
+    pr = [pr[i] + P["BIAS"].get(ops[i]["tag"], 0) + P["FINE"].get(ops[i]["fine"], 0) for i in range(n)]
+    free = dict(dve=0.0, act=0.0, pe=0.0, pool=0.0, sp=0.0)
+    free[None] = 0.0
+    order = dict((e, []) for e in free if e)
+    ready = dict((e, {}) for e in free)
+
+    def release(i):
+        o = ops[i]
+        r = 0.0
+        for j in o["hard"]:
+            r = max(r, ops[j]["end"] + (SL if ops[j]["eng"] == o["eng"] else XL))
+        for j in o["time"]:
+            r = max(r, ops[j]["end"])
+        ready[o["eng"]][i] = r
+
+    for i in range(n):
+        if left[i] == 0:
+            release(i)
+    for _ in range(n):
+        t0, e = min([(max(free[e], min(ready[e].values())), e) for e in ready if ready[e]], key=lambda x: x[0])
+        look = t0 + (LOOK if e in ("dve", "act") else 40)
+        i = max([i for i in ready[e] if ready[e][i] <= look], key=lambda i: (pr[i] - 2 * max(0, ready[e][i] - t0), -i))
+        t = max(t0, ready[e].pop(i))
+        o = ops[i]
+        o["start"], o["end"] = t, t + o["cost"] + o["lat"]
+        if e:
+            free[e] = t + o["cost"]
+            order[e].append(i)
+        for j in succ[i]:
+            left[j] -= 1
+            if left[j] == 0:
+                release(j)
+    if P.get("FAST"):
+        return None, order, None, ops
+    need = set(j for o in ops for j in o["hard"])
+    total = {}
+    for e in order:
+        for i in order[e]:
+            o = ops[i]
+            o["tok"] = None
+            if o["kind"] == "dma":
+                o["tok"] = (o["sem"], 16)
+                total[o["sem"]] = 16
+            elif o["kind"] != "send" and i in need:
+                total["s_" + e] = total.get("s_" + e, 0) + 1
+                o["tok"] = ("s_" + e, total["s_" + e])
+    for o in ops:
+        if o["kind"] == "recv":
+            o["tok"] = (o["sem"], -1)
+            o["know"] = {}
+    known = dict((e, {}) for e in order)
+    seq = sorted([o for o in ops if o["eng"]], key=lambda x: (x["start"], x["i"]))
+    for o in seq:
+        kn = known[o["eng"]]
+        waits = {}
+        for j in sorted(o["hard"], key=lambda j: -ops[j]["start"]):
+            s, v = ops[j]["tok"]
+            if s in kn and kn[s] >= v:
+                continue
+            waits[s] = max(waits.get(s, v), v)
+            kn[s] = v
+            for s2, v2 in ops[j]["know"].items():
+                if s2 not in kn or kn[s2] < v2:
+                    kn[s2] = v2
+        o["waits"] = sorted(waits.items())
+        o["know"] = dict(kn)
+    return seq, order, total, ops
+
+
+_CACHE = []
+
+
+def rank_program(g, core, T, topo):
+    rank = T.rank_of(core)
+    if rank is None:
+        return
+    if not _CACHE:
+        _CACHE.append(schedule())
+    seq, order, total, ops = _CACHE[0]
+    n = len(T.cores)
+    dst = T.cores[(rank + HOP) % n]
+    src = T.cores[(rank - HOP) % n]
+
+    def lanes(a, b):
+        return topo.engines(a, b)[:8]
+
+    mask = sum(1 << e for e in lanes(core, dst))
+    n_in = len(lanes(src, core))
+    rid, pid, _ = topo.addr(dst)
+    Q = dict(dve=g.vector, act=g.scalar, pe=g.tensor, pool=g, sp=g.sync)
+    sent = 0
+    for o in seq:
+        e, k = o["eng"], o["kind"]
+        q = Q[e]
+        for s, v in o["waits"]:
+            q.wait_ge(T.sem[s], n_in if v < 0 else v)
+        if k == "send":
+            su, lu, arr = o["args"]
+            g.remote_dma(T[lu][:, :], T[su][:, :], T.sem[arr], T.sem.sent, pid, rid, mask)
+            sent += len(lanes(core, dst))
+            continue
+        if k == "dma":
+            out, in_ = o["args"](T)
+            q.dma_start(out, in_).then_inc(T.sem[o["sem"]], 16)
+            continue
+        a = [_ap(T, x) for x in o["args"]]
+        if k == "cp":
+            ins = q.tensor_copy(a[0], a[1]) if e == "dve" else q.activation(a[0], a[1], AF.Copy)
+        elif k == "ts":
+            ins = q.tensor_scalar(*a[:5]) if a[5] is None else q.tensor_scalar(*a)
+        elif k == "tt":
+            ins = q.tensor_tensor(*a)
+        elif k == "scan":
+            ins = q.tensor_tensor_scan(*a)
+        elif k == "ms":
+            ins = q.memset(*a)
+        elif k == "act":
+            ins = q.activation(a[0], a[1], a[2], bias=a[3], scale=a[4])
+        elif k == "mm":
+            ins = q.matmul(*a)
+        elif BUF[o["args"][0][0]][2] == I:
+            ins = g.iota(*a)
+        else:
+            ins = g.iota(*a, allow_small_or_imprecise_dtypes=True)
+        if o["tok"] is not None:
+            ins.then_inc(T.sem[o["tok"][0]], 1)
+    for s in sorted(total):
+        g.wait_ge(T.sem[s], total[s])
+    for s in ARRS:
+        g.wait_ge(T.sem[s], n_in)
+    g.wait_ge(T.sem.sent, sent)

@@ -5,22 +5,27 @@ HS, HO = (128, 64), (0, 128)
 R = 2
 NS = 16 // R
 SUB = 4
-P = dict(PEF=0.55, GF=1.55, OV=20, XL=130, SL=70, SEND=3000, EQA=(1, 2), LOOK=60,
-         BIAS={'C0': 46300, 'F0': 8000, 'T0': 48100, 'G': 9000, 'D': 47300, 'L': 11700, 'X0': 13700, 'E0': 19300,
-               'M0': 10700, 'V0': 9700, 'W0': 24400, 'V1': 8900, 'W1': 25000, 'H': 55300, 'K': -1100, 'F1': -700,
-               'T1': 40600, 'X1': 10800, 'C1': -8700, 'E1': 30000, 'P0': 2600, 'P1': -4000, 'M1': 8400, 'U1': -4500,
-               'U0': -2000, 'Y0': 7100, 'Y1': 6700},
-         DG=[[2, 9, 0, 5, 1, 8], [3, 1, 9, 2, 1, 0], [3, 8, 0, 7, 4, 0]],
-         FINE={'W0pv': 500, 'C1cx': 6500, 'Huw': -5000, 'C0cx': 500, 'P0ms': 5000, 'M0me': -7000, 'P0tl': 2000,
-               'T0pa': 5500, 'P1zc': 2000, 'E1py': 9500, 'T1nw': -1500, 'W0ab': -5000, 'Dai': -2000, 'T0su': -4000,
-               'P0ks': -5000, 'Gag': -7000, 'V1pv': 5500, 'Gsg': -5000, 'V0pv': 500, 'T0': -5000, 'P1tt': -2000,
-               'Hof': 7000, 'Y1lf': -3000, 'U1un': -4000, 'Y0lf': 2000, 'Dun': 500, 'Ht1': 500, 'Hsc': -500,
-               'T1mk': 4000, 'X0lu': 5000, 'Ddv': -1500, 'F0pa': -3000, 'P1ks': 3500, 'W0vs': 2000, 'C0au': 500,
-               'F1pa': 2500, 'Hpv': 2000, 'W1hj': 4500, 'W0hc': 500, 'X1lu': 500, 'C1aa': 1500, 'W1hi': -8000,
-               'T1': -10000, 'W1ev': 1500, 'P1tl': 2000, 'W1hs': 7500, 'D': 500, 'W0mh': 2000, 'Heq': 5000,
-               'P0pg': 1500, 'W0hr': -5000, 'W0hs': -5000, 'W1mh': -7500, 'Ht2': 2000, 'U0un': -5500, 'T1su': -1000,
-               'Gpg': 4000, 'W0hj': -2000, 'W0ev': -1500, 'W0pd': 500, 'C1au': 2000, 'Y0l4': -2500, 'E0pa': -2000,
-               'X0x0': 500, 'Daj': -5000, 'P1pu': -500, 'T0mk': 1000, 'T0nw': 2000, 'P0tt': -500})
+P = dict(PEF=0.5, GF=1.55, OV=30, XL=220, SL=135, SEND=4500, EQA=(2, 2), EQH=2, LOOK=0,
+         EN=['act', 'act', 'dve', 'dve', 'act', 'act', 'act'],
+         BIAS={'C0': 75300, 'F0': 18900, 'T0': 56100, 'G': 14400, 'D': 27300, 'L': 22200, 'X0': 22100, 'E0': 46700,
+               'M0': 3300, 'V0': 39400, 'W0': 12700, 'V1': 9800, 'W1': 20400, 'H': 48200, 'K': 300, 'F1': 9000,
+               'T1': 38200, 'X1': 5100, 'C1': -11700, 'E1': 27000, 'P0': -19400, 'P1': 24700, 'M1': 600, 'U1': -29100,
+               'U0': 4500, 'Y0': 1100, 'Y1': 6100},
+         DG=[[2, 8, 1, 12, 1, 11], [3, 1, 12, 13, 1, 0], [9, 7, 12, 11, 8, 0]],
+         FINE={'C1au': -7000, 'P1ks': 6500, 'U0un': -2500, 'F0pa': -3500, 'T0su': 500, 'Hof': 2500, 'P1tt': 3000,
+               'E1py': -7000, 'F1mf': 10000, 'Huw': 2000, 'Ddv': 2000, 'P1pg': 500, 'P1zc': 5500, 'P0tt': 5000,
+               'M1me': 500, 'M0ys': -3500, 'F1pa': 7000, 'U0py': -5500, 'Lt5': 7000, 'C0cx': 10000, 'Lt3': 3500,
+               'T1su': 2000, 'W1hs': 2000, 'W0ev': 5000, 'W0mh': 1000, 'Hpv': 2500, 'C0aa': -4000, 'W1hr': -6500,
+               'W1pv': 500, 'W1hi': 1500, 'T0pa': 500, 'Daj': 4500, 'Gsg': -2000, 'P0ks': -4000, 'P1ms': 5000,
+               'V0pv': 7000, 'E0pa': -2000, 'T0mk': 1500, 'X1x1': 7500, 'W1vs': 8500, 'T1nw': 1500, 'Heq': -500,
+               'W0zz': -500, 'P1tl': 3000, 'W0hj': 4500, 'Ht0': -3500, 'Llw': -1500, 'X0lu': -7500, 'Gpg': -3000,
+               'Y0l4': 3000, 'T0nw': -9000, 'Gpv': -4000, 'Y1uw': 7000, 'P0pg': -10000, 'C0au': 4000, 'W1zz': -3000,
+               'M1ys': 3000, 'W1mh': 1000, 'Hsc': 5000, 'Lsc': -500, 'W0hr': 500, 'C1cx': -2500, 'W0hc': 5000,
+               'Geq': 7000, 'Y0lf': -5500, 'Ht1': -500, 'Hhp': 2000, 'T1': -5500, 'W1hj': -500, 'W0vs': 10000,
+               'M1pa': 500, 'P0tl': -2000, 'D': -500, 'Dun': -5500, 'C1aa': -500, 'Ht2': -2000, 'Lof': 2000,
+               'W0hi': 2000, 'W1ev': -7000, 'T1mk': 2500, 'Y1l4': -5000, 'W0hs': -3000, 'W0pv': -5000, 'Dai': 500,
+               'T1pa': 4500, 'P1pa': 5000, 'W0ac': -5000, 'Gpd': -5000, 'X0x0': 2000, 'M0me': 2000, 'T0': -2000,
+               'P1pu': 2000, 'W1pd': 2000, 'F0mf': -500})
 MAGIC = 12582912.0
 F, B, I, U = "float32", "bfloat16", "int32", "uint16"
 
@@ -43,7 +48,8 @@ def _sb(name, n, dt, where="sbuf"):
 
 
 for _n, _w, _d in [
-    ("xw", 2 * W, B), ("nbw", W, I), ("lw", W + S, B), ("tri", S, I), ("lbi", 256, I), ("lbb", 256, B), ("thi", 4, I),
+    ("xw", 2 * W, B), ("nbw", W, I), ("lw", W + S, F), ("tri", S, I), ("lbi", 256, I), ("lbb", 256, F), ("jrf", S, F),
+    ("thi", 4, I),
     ("jrow", S, B), ("pci", 4, I), ("pki", 4, I), ("pgi", 4, I), ("p1i", 4, I), ("p2i", 4, I), ("cols", 24, F),
     ("qg", 128, B), ("qk", S, B), ("q2", 128, B), ("q8", 64, B), ("kci", 64, B), ("kcc", 64, B), ("prf", 64, F),
     ("prb", 64, B), ("par", 128, B), ("ibc", 64, B), ("czi", 8, I), ("cz", 8, U),
@@ -56,7 +62,8 @@ for _n, _w, _d in [
     ("nthr", S, B), ("sg", S, B), ("pick", S, F), ("pik2", S, F), ("pik5", S, F),
     ("lf0", S, F), ("lf1", S, F), ("l4", S, F), ("unb", S, F), ("uw", 2 * S, F), ("pu", S, U), ("pgs", S, F),
     ("pgu", 12, U), ("pgf", 12, F), ("hi", S, I), ("hj", S, I), ("hrs", S, B), ("hsc", S, F), ("hc", 12, F),
-    ("hp", 12, F), ("eqh", 1248, B), ("eqp", 1248, B), ("sc", S, F), ("t0", 12, F), ("t1", 12, F), ("t2", 12, F),
+    ("hp", 12, F), ("eqh", 1248, B), ("eqd", 704, F), ("nwc", 12, F), ("eqp", 1248, B), ("sc", S, F), ("t0", 12, F),
+    ("t1", 12, F), ("t2", 12, F),
     ("offu", 12, U), ("ag", S, B), ("agd", 128, B), ("scp", S, F), ("t3", 12, F), ("t4", 12, F), ("t5", 12, F),
     ("ofp", 12, U), ("un", S, F), ("ai", S, I), ("aj", S, I), ("dv", S, F), ("ksc", 64, F), ("zc", 128, F),
     ("mkc", 64, B),
@@ -160,7 +167,7 @@ def build():
         return add("dve", "ms", (out, val), [out], [], OV + max(64, _n(out) * (0.5 if _two(out) else 1)))
 
     def act(out, a, fn, bias, scale=1.0):
-        return add("act", "act", (out, a, fn, bias, scale), [out], [a, bias], vcost(out, [a], 1))
+        return add("act", "act", (out, a, fn, bias, scale), [out], [a, bias, scale], vcost(out, [a], 1))
 
     def mm(out, l, r, st, sp):
         c = max(min(64, _n(l)), _n(r)) * (4 if BUF[l[0]][2] == F else 1) * P["PEF"] + 4
@@ -175,7 +182,9 @@ def build():
     col = lambda j, p=128: A("cols", j, j + 1, 1, p)
     PF, PK, PG, P16, M0, KM, KH, TH, G16, C1, C4096, PK4, PK2, PK5, PK6, P1, PH, KP, MB, P7 = range(20)
 
-    ms(A("lw"), 0.0)
+    ms(A("lw", 0, 536), 0.0)
+    for u in range(1, 8):
+        cp(A("lw", 536 * u, 536 * u + 536), A("lw", 0, 536), "act")
     ld = [dma("sp", "d_tr", lambda T: (T.tri[:, :], T.tr[:, :]), [A("tri")], [], 2400),
           dma("sp", "d_lb", lambda T: (T.lbi[:, :], T.lb[:, :]), [A("lbi")], [], 2400),
           dma("sp", "d_xs", lambda T: (T.xw[:, 0:W], T.xs[:, :]), [A("xw", 0, W)], [], 6500),
@@ -260,6 +269,8 @@ def build():
     ts(A("nthd"), A("thd"), -1.0, None, AL.mult)
     tt(A("wtmp"), A("wrow"), A("diag"), AL.mult)
     scan(A("wsc"), A("seg0"), A("wtmp"), 0.0, AL.mult, AL.max)
+    ts(A("nwc"), A("wsc", 15, S, 16), -1.0, None, AL.mult)
+    cp(A("jrf"), A("jrow"), "act")
     cp(A("c15"), A("c15i"))
     cp(A("uw", S, 2 * S), A("zero"), "act")
     for n in ("ks1", "ms1", "mh1"):
@@ -314,13 +325,17 @@ def build():
         if last is not None:
             mm(A(pa, 128, 256, 1, h), last, A("ibig"), False, True)
 
-    def firsts(eq, row, scal, bank, less):
+    def firsts(eq, row, scal, bank, less, on_act):
         o = 0
         mm(A(bank, 256, 448), A("ib"), A(less), True, False)
         for hh in range(12):
             n = S - 16 * hh
-            ts(A(eq, o, o + n), A(row, 16 * hh, S), A(scal, hh, hh + 1), A("wsc", 16 * hh + 15, 16 * hh + 16),
-               AL.is_equal, AL.mult)
+            w = A("wsc", 16 * hh + 15, 16 * hh + 16)
+            if hh < on_act:
+                act(A("eqd", o, o + n), A(row, 16 * hh, S), AF.Abs, A(scal, hh, hh + 1), -1.0)
+                act(A(eq, o, o + n), A("eqd", o, o + n), AF.Relu, w, A("nwc", hh, hh + 1))
+            else:
+                ts(A(eq, o, o + n), A(row, 16 * hh, S), A(scal, hh, hh + 1), w, AL.is_equal, AL.mult)
             mm(A(bank, 256 + 16 * hh, 448), A("bob"), A(eq, o, o + n), False, hh == 11)
             o += n
 
@@ -358,13 +373,13 @@ def build():
             et = A(pa, 128, 256, 1, h)
             kl, kr = A(n("ks"), p=h), A("idf", 0, h, 1, h)
             if c == 1:
-                cp(A("ksc"), A(pa, 128, 192), "act")
+                cp(A("ksc"), A(pa, 128, 192), P["EN"][6])
                 tt(A("zc"), IND(A("ksc"), A("cz")), A("par"), AL.mult)
                 et = A(pa, 256, 384, 1, h)
                 mm(et, A("prf"), A("zc"), True, True)
                 kl, kr = A("zc"), A("prf")
             scan(A(n("ms"), p=h), A("rst", p=h), et, 0.0, AL.add, AL.min)
-            cp(A(n("ks"), p=h), et, "act")
+            cp(A(n("ks"), p=h), et, P["EN"][c])
             tt(A(n("tt")), IND(A(n("ms")), A("c15")), A(n("ks")), AL.is_equal)
             mm(A(pa, 0, h), A(n("tt"), p=h), A("ib", 0, h, 1, h), True, True)
             tag[0] = "U%d" % c
@@ -385,7 +400,7 @@ def build():
             for k in range(16):
                 mm(A(pv, 0, h), A("wbig", 16 - k, 144 - k), A(n("v"), k, None, 16), k == 0, k == 15)
             tag[0] = "W%d" % c
-            cp(A(n("vs")), A(pv, 0, h), "act")
+            cp(A(n("vs")), A(pv, 0, h), P["EN"][2 + c])
             tt(A(n("ev"), 8 * h, 9 * h), A(pv, 0, h), H("jrow", c), AL.is_equal)
             for s in range(8):
                 mm(A("pd%d" % (s // 4), h * (s % 4), h * (s % 4 + 1)), A("dm_s", 128 * s, 128 * s + 128), A(n("vs")), True, True)
@@ -403,7 +418,7 @@ def build():
             for s in range(8):
                 mm(kt, A(n("ev"), h * s, h * s + h), A("rm_s", 128 * s, 128 * s + 128), False, s == 7)
             scan(A(n("mh"), p=h), A("seg0", 0, 128, 1, h), kt, 0.0, AL.mult, AL.max)
-            cp(A(n("zz")), IND(A(n("mh")), A("c15")), "act")
+            cp(A(n("zz")), IND(A(n("mh")), A("c15")), P["EN"][4 + c])
             mm(A(pv, 256, 256 + h), A(n("zz"), p=h), A("idf", 0, h, 1, h), True, True)
             cp(H("hi", c), A(pv, 256, 256 + h))
             ts(H("hj", c), H("hi", c), 511, None, AL.bitwise_and)
@@ -412,7 +427,7 @@ def build():
             ts(G("hc", c), E15("hsc", c), col(PK5), None, AL.add)
         tag[0] = "H"
         ts(A("hp"), A("hsc", 15, S, 16), col(PK6), None, AL.add)
-        firsts("eqh", "hrs", "hc", "pv0", "nthd")
+        firsts("eqh", "hrs", "hc", "pv0", "nthd", P["EQH"])
         scan(A("sc"), A("seg0"), A("pv0", 256, 448), 0.0, AL.mult, AL.max)
         ts(A("t0"), A("sc", 15, S, 16), 0.0, 1024.0, AL.is_gt, AL.mult)
         tt(A("t1"), A("t0"), A("j192"), AL.min)
@@ -426,7 +441,7 @@ def build():
             gather("cx%d" % c, A("xw"), "au%d" % c, t, 4 + c)
         tag[0] = "G"
         ts(A("pgf"), A("pgs", 15, S, 16), col(PK4), None, AL.add)
-        firsts("eqp", "pu", "pgf", "pv1", "nthr")
+        firsts("eqp", "pu", "pgf", "pv1", "nthr", 0)
         act(A("sg"), A("pv1", 256, 448), AF.Sign, 0.0)
         act(A("pd0", 0, S), A("sg"), AF.Relu, 0.0, -1.0)
         act(A("ag"), A("sg"), AF.Relu, 0.0)
@@ -439,14 +454,14 @@ def build():
         tt(A("t3"), A("t5"), A("j4096"), AL.min)
         tt(A("t4"), A("t3"), A("pgf"), AL.max)
         cp(A("ofp"), A("t4"))
-        cp(IND(A("lw"), A("ofp")), A("jrow"))
+        cp(IND(A("lw"), A("ofp")), A("jrf"))
         tag[0] = "D"
         tt(A("un"), A("uw", 0, S), A("pd0", 0, S), AL.mult)
         tt(A("ai"), IND(A("nbw"), A("pgu")), A("un"), AL.max)
         ts(A("aj"), A("ai"), 4095, None, AL.bitwise_and)
         tt(A("dv"), A("aj"), A("pd0", S, 2 * S), AL.subtract)
         if t == ST - 1:
-            dma("pool", "d_yb", lambda T: (T.yb[:, :], T.lw[0:128:16, 0:W]), [], [A("lw", 0, W)], 4500)
+            dma("sp", "d_yb", lambda T: (T.yb[:, :], T.lw[0:128:16, 0:W]), [], [A("lw", 0, W)], 4500)
         for c in range(2):
             n = lambda s: "%s%d" % (s, c)
             pa, h = n("pa"), HS[c]

@@ -5,33 +5,45 @@ HS, HO = (128, 64), (0, 128)
 R = 2
 NS = 16 // R
 SUB = 4
-P = dict(PEF=0.5, GF=1.55, OV=30, XL=220, SL=135, SEND=4500, EQA=(2, 2), EQH=2, LOOK=0,
-         EN=['act', 'act', 'dve', 'dve', 'act', 'act', 'act'],
-         BIAS={'C0': 75300, 'F0': 18900, 'T0': 56100, 'G': 14400, 'D': 27300, 'L': 22200, 'X0': 22100, 'E0': 46700,
-               'M0': 3300, 'V0': 39400, 'W0': 12700, 'V1': 9800, 'W1': 20400, 'H': 48200, 'K': 300, 'F1': 9000,
-               'T1': 38200, 'X1': 5100, 'C1': -11700, 'E1': 27000, 'P0': -19400, 'P1': 24700, 'M1': 600, 'U1': -29100,
-               'U0': 4500, 'Y0': 1100, 'Y1': 6100},
-         DG=[[2, 8, 1, 12, 1, 11], [3, 1, 12, 13, 1, 0], [9, 7, 12, 11, 8, 0]],
-         FINE={'C1au': -7000, 'P1ks': 6500, 'U0un': -2500, 'F0pa': -3500, 'T0su': 500, 'Hof': 2500, 'P1tt': 3000,
-               'E1py': -7000, 'F1mf': 10000, 'Huw': 2000, 'Ddv': 2000, 'P1pg': 500, 'P1zc': 5500, 'P0tt': 5000,
-               'M1me': 500, 'M0ys': -3500, 'F1pa': 7000, 'U0py': -5500, 'Lt5': 7000, 'C0cx': 10000, 'Lt3': 3500,
-               'T1su': 2000, 'W1hs': 2000, 'W0ev': 5000, 'W0mh': 1000, 'Hpv': 2500, 'C0aa': -4000, 'W1hr': -6500,
-               'W1pv': 500, 'W1hi': 1500, 'T0pa': 500, 'Daj': 4500, 'Gsg': -2000, 'P0ks': -4000, 'P1ms': 5000,
-               'V0pv': 7000, 'E0pa': -2000, 'T0mk': 1500, 'X1x1': 7500, 'W1vs': 8500, 'T1nw': 1500, 'Heq': -500,
-               'W0zz': -500, 'P1tl': 3000, 'W0hj': 4500, 'Ht0': -3500, 'Llw': -1500, 'X0lu': -7500, 'Gpg': -3000,
-               'Y0l4': 3000, 'T0nw': -9000, 'Gpv': -4000, 'Y1uw': 7000, 'P0pg': -10000, 'C0au': 4000, 'W1zz': -3000,
-               'M1ys': 3000, 'W1mh': 1000, 'Hsc': 5000, 'Lsc': -500, 'W0hr': 500, 'C1cx': -2500, 'W0hc': 5000,
-               'Geq': 7000, 'Y0lf': -5500, 'Ht1': -500, 'Hhp': 2000, 'T1': -5500, 'W1hj': -500, 'W0vs': 10000,
-               'M1pa': 500, 'P0tl': -2000, 'D': -500, 'Dun': -5500, 'C1aa': -500, 'Ht2': -2000, 'Lof': 2000,
-               'W0hi': 2000, 'W1ev': -7000, 'T1mk': 2500, 'Y1l4': -5000, 'W0hs': -3000, 'W0pv': -5000, 'Dai': 500,
-               'T1pa': 4500, 'P1pa': 5000, 'W0ac': -5000, 'Gpd': -5000, 'X0x0': 2000, 'M0me': 2000, 'T0': -2000,
-               'P1pu': 2000, 'W1pd': 2000, 'F0mf': -500})
+P = dict(PEF=0.5, GF=1.55, OV=30, XL=220, SL=135, SEND=4500, EQA=(2, 2), EQH=2, AG=[0, 0, 1], TRIES=450,
+         EN=['dve', 'act', 'dve', 'dve', 'dve', 'act', 'act'],
+         BIAS={'C0': 92000, 'F0': 14900, 'T0': 22800, 'G': 18300, 'D': 23000, 'L': 13400, 'X0': 21800, 'E0': 32300,
+               'M0': 4000, 'V0': 89300, 'W0': 20100, 'V1': -800, 'W1': 20600, 'H': 66100, 'K': -400, 'F1': 6000,
+               'T1': 53900, 'X1': -3000, 'C1': -32400, 'E1': 40100, 'P0': -11300, 'P1': 37200, 'M1': 8500,
+               'U1': -33400, 'U0': -23600, 'Y0': 2300, 'Y1': -20300},
+         DG=[[10, 8, 1, 6, 1, 0], [3, 9, 12, 9, 5, 1], [9, 6, 12, 6, 0, 4]],
+         FINE={'C1au': -3000, 'P1ks': 8500, 'U0un': -1000, 'F0pa': -4000, 'T0su': 1000, 'Hof': 3000, 'P1tt': -500,
+               'E1py': -2000, 'F1mf': 11500, 'Huw': 7000, 'P1pg': 500, 'P1zc': 5500, 'P0tt': 3000, 'M1me': 500,
+               'M0ys': 1500, 'F1pa': 7000, 'C0cx': 11500, 'T1su': -1000, 'W1hs': -1500, 'W0ev': 7500, 'W0mh': 4000,
+               'C0aa': -1000, 'W1hr': -6500, 'W1pv': 500, 'W1hi': 1500, 'T0pa': 5000, 'Daj': 6000, 'Gsg': -2000,
+               'P0ks': -4000, 'P1ms': 6500, 'V0pv': 9000, 'E0pa': -1500, 'T0mk': -1500, 'X1x1': 10000, 'W1vs': 8500,
+               'T1nw': 1000, 'Heq': -3500, 'W0zz': 9000, 'P1tl': -1500, 'W0hj': 9500, 'Ht0': -6000, 'Llw': -1500,
+               'X0lu': -7500, 'Gpg': -13500, 'Y0l4': 3000, 'T0nw': -9000, 'Gpv': -6000, 'P0pg': -13000, 'C0au': 6000,
+               'W1zz': -2500, 'M1ys': 4500, 'W1mh': -2500, 'Hsc': 10000, 'Lsc': -1000, 'W0hr': -6500, 'W0hc': 500,
+               'Geq': 7000, 'Y0lf': -6500, 'T1': -12000, 'W0vs': 10000, 'M1pa': -5500, 'P0tl': -3500, 'D': -5500,
+               'Dun': -5500, 'C1aa': -1000, 'Ht2': -7000, 'Lof': 2500, 'W1ev': -7000, 'T1mk': -1500, 'Y1l4': -5500,
+               'W0hs': -4500, 'W0pv': -4500, 'Dai': -6500, 'T1pa': 6500, 'P1pa': 15000, 'W0ac': -5000, 'Gpd': -5500,
+               'X0x0': 5500, 'M0me': -500, 'T0': -2000, 'P1pu': 3500, 'W1pd': 2000, 'F0mf': 9500, 'T0n2': -4500,
+               'E0py': 6500, 'W0ab': 9500, 'Gag': 9500, 'Y1lf': -5000, 'P0pa': -500, 'Lt4': -5500, 'T1n2': -5500,
+               'U1un': -4500, 'P0pu': 5500, 'V1pv': 4000, 'E1pa': 2000, 'U1py': 9000, 'W1ac': -500, 'P0ms': 1500,
+               'V0v0': 2500, 'W1ab': -5500, 'V1v1': 2000},
+         SB={'La': -44000, 'Hb': 2000, 'T0c': 16000, 'E0c': -8000, 'E1a': -24000, 'U1b': 16000, 'T0a': 4000, 'Ga': 15000,
+             'P1b': -13000, 'W1b': 8000, 'C0a': 9000, 'P1a': -3000, 'C0c': 7000, 'X1c': -8000, 'X0a': -5000, 'U0a': 11000,
+             'W1a': 4000, 'Ha': -2000, 'C0b': -16000, 'M1c': 1000, 'Gb': 2000, 'V0c': -3000, 'E0b': 18000, 'V0b': 13000,
+             'T1a': -2000, 'Hc': 4000, 'U1c': -1000, 'V1a': 6000, 'T0b': 5000, 'E1c': 12000, 'P1c': 10000, 'X1b': 4000,
+             'U0b': -7000, 'F0b': 1000, 'F1c': -2000, 'Lb': -15000, 'E0a': -12000, 'C1a': -8000, 'T1b': 8000,
+             'X0c': -8000, 'M0b': -5000, 'V0a': 21000, 'V1b': 12000, 'Y1c': -23000, 'X1a': -4000, 'Db': -4000,
+             'E1b': 12000, 'Y0a': -4000, 'W0c': -1000, 'F0a': 8000, 'Y0b': 1000, 'M1a': 1000, 'M1b': 12000, 'W0b': 12000,
+             'M0a': 3000, 'X0b': 8000, 'Y1b': -23000, 'U0c': 13000, 'W0a': 8000, 'P0b': 4000, 'Dc': -28000, 'V1c': 4000,
+             'C1b': -4000, 'Da': 16000, 'Lc': -1000, 'F1a': 1000})
+SETS = [(dict(XL=250, SL=150, SEND=4500), 105500), (dict(GF=2.0, XL=175, SL=105, SEND=3300), 107000),
+        (dict(GF=1.2, XL=210, SL=130, SEND=5000, PEF=0.55), 103000)]
 MAGIC = 12582912.0
 F, B, I, U = "float32", "bfloat16", "int32", "uint16"
 
 SCRATCH = {}
 BUF = {}
-POOLED = ("pci pki pgi p1i p2i sa sa2 sbi sb2 jgi c15i czi saf sbf rw i32f j192 j4096 half zero wrow wtmp wsc thr thd seg0 "
+POOLED = ("pci pki pgi p1i p2i sa sa2 sbi sb2 jgi c15i czi saf sbf rw i32f j192 j4096 half zero wrow wtmp wsc thd seg0 "
           "rst idf bof bom ib i16 bob kc kh i192 ibig ones qg qk im16 wbig diag cy nthd nthr pick pik2 pik5 kcc kci prf "
           "prb par q2 q8 ibc").split()
 
@@ -49,23 +61,21 @@ def _sb(name, n, dt, where="sbuf"):
 
 for _n, _w, _d in [
     ("xw", 2 * W, B), ("nbw", W, I), ("lw", W + S, F), ("tri", S, I), ("lbi", 256, I), ("lbb", 256, F), ("jrf", S, F),
-    ("thi", 4, I),
-    ("jrow", S, B), ("pci", 4, I), ("pki", 4, I), ("pgi", 4, I), ("p1i", 4, I), ("p2i", 4, I), ("cols", 24, F),
-    ("qg", 128, B), ("qk", S, B), ("q2", 128, B), ("q8", 64, B), ("kci", 64, B), ("kcc", 64, B), ("prf", 64, F),
-    ("prb", 64, B), ("par", 128, B), ("ibc", 64, B), ("czi", 8, I), ("cz", 8, U),
+    ("thi", 4, I), ("jrow", S, B), ("pci", 4, I), ("pki", 4, I), ("pgi", 4, I), ("p1i", 4, I), ("p2i", 4, I),
+    ("cols", 24, F), ("qg", 128, B), ("qk", S, B), ("q2", 128, B), ("q8", 64, B), ("kci", 64, B), ("kcc", 64, B),
+    ("prf", 64, F), ("prb", 64, B), ("par", 128, B), ("ibc", 64, B), ("czi", 8, I), ("cz", 8, U),
     ("ib", 128, B), ("idf", 128, F), ("bob", 128, B), ("bof", 128, F), ("bom", 128, F), ("i32f", 8, F), ("im16", 8, B),
     ("wbig", 144, B), ("pm_s", 1024, B), ("dm_s", 1024, B), ("rm_s", 1024, B), ("sa", 8, I), ("sa2", 8, I), ("saf", 8, F),
     ("sbi", 8, I), ("sb2", 8, I), ("sbf", 8, F), ("rw", 8, F), ("kc", 128, B), ("kh", 128, B), ("i192", 128, B),
     ("ibig", 128, B), ("ones", 128, B), ("diag", S, B), ("seg0", S, F), ("rst", 128, F), ("jgi", 12, I),
-    ("j192", 12, F), ("j4096", 12, F), ("half", S, F), ("zero", S, F), ("wrow", S, F), ("thr", S, F), ("thd", S, F),
+    ("j192", 24, F), ("j4096", 24, F), ("half", S, F), ("zero", S, F), ("wrow", S, F), ("thd", S, F),
     ("wtmp", S, F), ("wsc", S, F), ("c15i", 8, I), ("c15", 8, U), ("i16", 128, B), ("cy", 128, B), ("nthd", S, B),
     ("nthr", S, B), ("sg", S, B), ("pick", S, F), ("pik2", S, F), ("pik5", S, F),
     ("lf0", S, F), ("lf1", S, F), ("l4", S, F), ("unb", S, F), ("uw", 2 * S, F), ("pu", S, U), ("pgs", S, F),
-    ("pgu", 12, U), ("pgf", 12, F), ("hi", S, I), ("hj", S, I), ("hrs", S, B), ("hsc", S, F), ("hc", 12, F),
-    ("hp", 12, F), ("eqh", 1248, B), ("eqd", 704, F), ("nwc", 12, F), ("eqp", 1248, B), ("sc", S, F), ("t0", 12, F),
-    ("t1", 12, F), ("t2", 12, F),
-    ("offu", 12, U), ("ag", S, B), ("agd", 128, B), ("scp", S, F), ("t3", 12, F), ("t4", 12, F), ("t5", 12, F),
-    ("ofp", 12, U), ("un", S, F), ("ai", S, I), ("aj", S, I), ("dv", S, F), ("ksc", 64, F), ("zc", 128, F),
+    ("pgu", 12, U), ("pgf", 24, F), ("hi", S, I), ("hj", S, I), ("hrs", S, B), ("hsc", S, F), ("hc", 12, F),
+    ("eqh", 1248, B), ("eqd", 704, F), ("nwc", 12, F), ("eqp", 1248, B), ("sc", S, F), ("t0", 24, F), ("t2", 24, F),
+    ("offu", 12, U), ("ag", S, B), ("agd", 128, B), ("scp", S, F), ("t4", 24, F),
+    ("ofp", 12, U), ("un", S, F), ("ai", S, I), ("aj", S, I), ("dv", 2 * S, F), ("ksc", 64, F), ("zc", 128, F),
     ("mkc", 64, B),
 ]:
     _sb(_n, _w, _d)
@@ -74,7 +84,7 @@ for _c in range(2):
     for _n, _w, _d in [("x", 16 * _h, B), ("cx", 16 * _h, B), ("v", 16 * _h, B), ("me", 16 * _h, F), ("mf", 16 * _h, F),
                        ("ys", _h, F), ("ac", 4 * _h, B), ("ks", 128, F), ("ms", 128, F), ("tt", 128, B), ("tl", _h, F),
                        ("ab", 4 * _h, B), ("vs", _h, B), ("ev", 9 * _h, B), ("mh", 128, F), ("zz", 128, F),
-                       ("aa", _h, F), ("au", _h, U), ("mk", 128, B), ("nw", _h, F)]:
+                       ("aa", _h, F), ("au", _h, U), ("mk", 128, B), ("nw", _h, F), ("n2", 2 * _h, F)]:
         _sb("%s%d" % (_n, _c), _w, _d)
     for _t in range(ST):
         _sb("lu%d%d" % (_t, _c), _h, U)
@@ -121,8 +131,8 @@ def _two(a):
 
 def build():
     ops = []
-    OV, DG = P["OV"], P["DG"]
-    tag = ["K"]
+    OV = P["OV"]
+    tag = ["K", ""]
 
     def add(eng, kind, args, outs, ins, cost, **kw):
         rd, wr = [], []
@@ -136,6 +146,7 @@ def build():
             else:
                 wr.append(a)
         o = dict(tag=tag[0], eng=eng, kind=kind, args=args, rd=rd, wr=wr, cost=cost, extra=[], lat=0)
+        o["st"] = tag[0] + tag[1]
         o["fine"] = tag[0] + (wr[0][0][:2] if wr else "")
         o.update(kw)
         ops.append(o)
@@ -169,6 +180,9 @@ def build():
     def act(out, a, fn, bias, scale=1.0):
         return add("act", "act", (out, a, fn, bias, scale), [out], [a, bias, scale], vcost(out, [a], 1))
 
+    def scaled(out, a, s):
+        return act(A(out), A(a), AF.Identity, 0.0, s)
+
     def mm(out, l, r, st, sp):
         c = max(min(64, _n(l)), _n(r)) * (4 if BUF[l[0]][2] == F else 1) * P["PEF"] + 4
         return add("pe", "mm", (out, l, r, st, sp), [out], [l, r], c)
@@ -180,7 +194,7 @@ def build():
         return add(q, "dma", fn, outs, ins, 60, sem=sem, lat=lat)
 
     col = lambda j, p=128: A("cols", j, j + 1, 1, p)
-    PF, PK, PG, P16, M0, KM, KH, TH, G16, C1, C4096, PK4, PK2, PK5, PK6, P1, PH, KP, MB, P7 = range(20)
+    PF, PK, PG, P16, M0, KM, KH, TH, G16, C1, C4096, PK4, PK2, PK5, PK6, P1, PH, KP, MB, P7, C2, C512 = range(22)
 
     ms(A("lw", 0, 536), 0.0)
     for u in range(1, 8):
@@ -221,19 +235,21 @@ def build():
     ts(col(PK5), pk, 512.0, -7680.0, AL.mult, AL.add)
     ts(col(PK6), pk, 512.0, -7488.0, AL.mult, AL.add)
     ms(col(C1), 1.0)
+    ms(col(C2), 2.0)
+    ms(col(C512), 512.0)
     ms(col(C4096), 4096.0)
     j128 = A("jrow", 0, 128)
     ts(A("ib"), j128, col(PF), None, AL.is_equal)
-    ts(A("i16"), j128, col(PF), 0.0625, AL.is_equal, AL.mult)
+    scaled("i16", "ib", 0.0625)
     ms(A("cy"), -0.46875)
-    ts(A("idf"), j128, col(PF), None, AL.is_equal)
-    ts(A("kc"), j128, col(PF), col(KM), AL.is_equal, AL.mult)
-    ts(A("kh"), j128, col(PF), col(KH), AL.is_equal, AL.mult)
-    ts(A("i192"), j128, col(PF), 192.0, AL.is_equal, AL.mult)
-    ts(A("ibig"), j128, col(PF), -float(2 ** 26), AL.is_equal, AL.mult)
+    scaled("idf", "ib", 1.0)
+    scaled("kc", "ib", col(KM))
+    scaled("kh", "ib", col(KH))
+    scaled("i192", "ib", 192.0)
+    scaled("ibig", "ib", -float(2 ** 26))
     ts(A("bob"), A("qg"), col(PG), None, AL.is_equal)
-    ts(A("bof"), A("qg"), col(PG), None, AL.is_equal)
-    ts(A("bom"), A("qg"), col(PG), -16.0, AL.is_equal, AL.mult)
+    scaled("bof", "bob", 1.0)
+    scaled("bom", "bob", -16.0)
     ts(A("i32f"), A("jrow", 0, 8), col(PG), 32.0, AL.is_equal, AL.mult)
     ts(A("im16"), A("jrow", 0, 8), col(PG), -16.0, AL.is_equal, AL.mult)
     ts(A("wbig"), A("jrow", 0, 144), col(P16), col(M0), AL.is_equal, AL.mult)
@@ -253,26 +269,26 @@ def build():
         cp(A("dm_s", 512 * s, 512 * s + 512), A("pd%d" % s), "act")
     ms(A("ones"), 1.0)
     ts(A("diag"), A("qk"), col(PK), None, AL.is_equal)
-    for n, step in (("pick", 4096.0), ("pik2", 2.0), ("pik5", 512.0)):
-        ts(A(n), A("diag"), -float(2 ** 20), step, AL.mult, AL.add)
+    for n, step in (("pick", C4096), ("pik2", C2), ("pik5", C512)):
+        act(A(n), A("diag"), AF.Identity, col(step), -float(2 ** 20))
     ts(A("seg0"), A("qk"), 0.0, None, AL.not_equal)
     ts(A("rst"), A("qk", 0, 128), 0.0, float(2 ** 25), AL.is_equal, AL.mult)
-    ts(A("j192"), A("jgi"), col(PK), 192.0, AL.add, AL.add)
-    ts(A("j4096"), A("jgi"), col(PK), 4096.0, AL.add, AL.add)
+    for n, base in (("j192", 192.0), ("j4096", 4096.0)):
+        ms(A(n, 0, 24, 2), -65536.0)
+        ts(A(n, 1, 24, 2), A("jgi"), col(PK), base, AL.add, AL.add)
     ms(A("half"), 0.5)
     ms(A("zero"), 0.0)
     scan(A("wrow"), A("half"), A("zero"), float(2 ** 96), AL.mult, AL.add)
-    ts(A("thr"), A("wrow"), 2.5, None, AL.mult)
-    ts(A("wtmp"), A("qk"), col(PK), float(2 ** 98), AL.not_equal, AL.mult)
-    tt(A("thd"), A("wtmp"), A("thr"), AL.add)
-    ts(A("nthr"), A("wrow"), -2.5, None, AL.mult)
-    ts(A("nthd"), A("thd"), -1.0, None, AL.mult)
+    scaled("nthr", "wrow", -2.5)
+    ts(A("thd"), A("qk"), col(PK), -float(2 ** 98), AL.not_equal, AL.mult)
+    tt(A("nthd"), A("thd"), A("nthr"), AL.add)
     tt(A("wtmp"), A("wrow"), A("diag"), AL.mult)
     scan(A("wsc"), A("seg0"), A("wtmp"), 0.0, AL.mult, AL.max)
     ts(A("nwc"), A("wsc", 15, S, 16), -1.0, None, AL.mult)
     cp(A("jrf"), A("jrow"), "act")
     cp(A("c15"), A("c15i"))
     cp(A("uw", S, 2 * S), A("zero"), "act")
+    cp(A("dv", 0, 2 * S, 2), A("zero"), "act")
     for n in ("ks1", "ms1", "mh1"):
         cp(A(n), A("zero", 0, 128), "act")
     iota(A("q2"), [[0, 8], [1, 2], [0, 8]], 0, 0)
@@ -288,8 +304,8 @@ def build():
     ts(col(KP), A("p1i", 0, 1), 8.0, -15.0, AL.mult, AL.add)
     ts(col(MB), pk, 0.0, -float(2 ** 26), AL.is_equal, AL.mult)
     ts(A("kcc"), A("kci"), col(KP), None, AL.add)
-    ts(A("prf"), A("jrow", 0, 64), col(PH), None, AL.is_equal)
     ts(A("prb"), A("jrow", 0, 64), col(PH), None, AL.is_equal)
+    scaled("prf", "prb", 1.0)
     ts(A("par"), A("q2"), col(P1), None, AL.is_equal)
     ts(A("ibc"), A("q8"), col(PG), col(MB), AL.is_equal, AL.mult)
     ts(A("cz"), A("czi"), col(P7), None, AL.add)
@@ -297,9 +313,7 @@ def build():
     def gather(dst, win, off, t, j):
         q = HS[j % 2] // SUB
         for u in range(SUB):
-            o = cp(A(dst, 16 * q * u, 16 * q * (u + 1)), IND(win, A(off, q * u, q * (u + 1))),
-                   "dve" if DG[t][j] >> u & 1 else "act")
-            o["gat"] = (t, j, u)
+            cp(A(dst, 16 * q * u, 16 * q * (u + 1)), IND(win, A(off, q * u, q * (u + 1))), "act")["gat"] = (t, j, u)
 
     def energy(c, x, m, last):
         pa, py, h = "pa%d" % c, "py%d" % c, HS[c]
@@ -332,10 +346,10 @@ def build():
             n = S - 16 * hh
             w = A("wsc", 16 * hh + 15, 16 * hh + 16)
             if hh < on_act:
-                act(A("eqd", o, o + n), A(row, 16 * hh, S), AF.Abs, A(scal, hh, hh + 1), -1.0)
+                act(A("eqd", o, o + n), A(row, 16 * hh, S), AF.Abs, scal(hh), -1.0)
                 act(A(eq, o, o + n), A("eqd", o, o + n), AF.Relu, w, A("nwc", hh, hh + 1))
             else:
-                ts(A(eq, o, o + n), A(row, 16 * hh, S), A(scal, hh, hh + 1), w, AL.is_equal, AL.mult)
+                ts(A(eq, o, o + n), A(row, 16 * hh, S), scal(hh), w, AL.is_equal, AL.mult)
             mm(A(bank, 256 + 16 * hh, 448), A("bob"), A(eq, o, o + n), False, hh == 11)
             o += n
 
@@ -345,6 +359,7 @@ def build():
     sends = {}
     for t in range(ST):
         lf = "lf%d" % (t % 2)
+        tag[1] = "abc"[t]
         for c in range(2):
             lu = "lu%d%d" % (t, c)
             tag[0] = "X%d" % c
@@ -426,13 +441,12 @@ def build():
             scan(H("hsc", c), A("pik5", 0, h), H("hrs", c), 0.0, AL.add, AL.max)
             ts(G("hc", c), E15("hsc", c), col(PK5), None, AL.add)
         tag[0] = "H"
-        ts(A("hp"), A("hsc", 15, S, 16), col(PK6), None, AL.add)
-        firsts("eqh", "hrs", "hc", "pv0", "nthd", P["EQH"])
+        ts(A("t0", 1, 24, 2), A("hsc", 15, S, 16), col(PK6), None, AL.add)
+        firsts("eqh", "hrs", lambda hh: A("hc", hh, hh + 1), "pv0", "nthd", P["EQH"])
         scan(A("sc"), A("seg0"), A("pv0", 256, 448), 0.0, AL.mult, AL.max)
-        ts(A("t0"), A("sc", 15, S, 16), 0.0, 1024.0, AL.is_gt, AL.mult)
-        tt(A("t1"), A("t0"), A("j192"), AL.min)
-        tt(A("t2"), A("t1"), A("hp"), AL.max)
-        cp(A("offu"), A("t2"))
+        ts(A("t0", 0, 24, 2), A("sc", 15, S, 16), 0.0, 1024.0, AL.is_gt, AL.mult)
+        scan(A("t2"), A("j192"), A("t0"), 0.0, AL.min, AL.max)
+        cp(A("offu"), A("t2", 1, 24, 2))
         tt(IND(A("uw"), A("offu")), A("unb"), A("l4"), AL.mult)
         for c in range(2):
             tag[0] = "C%d" % c
@@ -440,49 +454,53 @@ def build():
             cp(A("au%d" % c), A("aa%d" % c))
             gather("cx%d" % c, A("xw"), "au%d" % c, t, 4 + c)
         tag[0] = "G"
-        ts(A("pgf"), A("pgs", 15, S, 16), col(PK4), None, AL.add)
-        firsts("eqp", "pu", "pgf", "pv1", "nthr", 0)
-        act(A("sg"), A("pv1", 256, 448), AF.Sign, 0.0)
-        act(A("pd0", 0, S), A("sg"), AF.Relu, 0.0, -1.0)
-        act(A("ag"), A("sg"), AF.Relu, 0.0)
+        ts(A("pgf", 1, 24, 2), A("pgs", 15, S, 16), col(PK4), None, AL.add)
+        firsts("eqp", "pu", lambda hh: A("pgf", 2 * hh + 1, 2 * hh + 2), "pv1", "nthr", 0)
         cp(A("pd0", S, 2 * S), A(lf), "act")
+        if P["AG"][t]:
+            ts(A("pd0", 0, S), A("pv1", 256, 448), 0.0, None, AL.is_lt)
+            ts(A("ag"), A("pv1", 256, 448), 0.0, None, AL.is_gt)
+        else:
+            act(A("sg"), A("pv1", 256, 448), AF.Sign, 0.0)
+            act(A("pd0", 0, S), A("sg"), AF.Relu, 0.0, -1.0)
+            act(A("ag"), A("sg"), AF.Relu, 0.0)
         for a in range(2):
             cp(A("agd", a, 128, 2), H("ag", 1), "act")
         tag[0] = "L"
         scan(A("scp"), A("pik2"), A("ag"), 0.0, AL.add, AL.max)
-        ts(A("t5"), A("scp", 15, S, 16), col(PK2), 8192.0, AL.add, AL.mult)
-        tt(A("t3"), A("t5"), A("j4096"), AL.min)
-        tt(A("t4"), A("t3"), A("pgf"), AL.max)
-        cp(A("ofp"), A("t4"))
+        ts(A("pgf", 0, 24, 2), A("scp", 15, S, 16), col(PK2), 8192.0, AL.add, AL.mult)
+        scan(A("t4"), A("j4096"), A("pgf"), 0.0, AL.min, AL.max)
+        cp(A("ofp"), A("t4", 1, 24, 2))
         cp(IND(A("lw"), A("ofp")), A("jrf"))
         tag[0] = "D"
         tt(A("un"), A("uw", 0, S), A("pd0", 0, S), AL.mult)
         tt(A("ai"), IND(A("nbw"), A("pgu")), A("un"), AL.max)
         ts(A("aj"), A("ai"), 4095, None, AL.bitwise_and)
-        tt(A("dv"), A("aj"), A("pd0", S, 2 * S), AL.subtract)
+        tt(A("dv", 1, 2 * S, 2), A("aj"), A("pd0", S, 2 * S), AL.subtract)
         if t == ST - 1:
             dma("sp", "d_yb", lambda T: (T.yb[:, :], T.lw[0:128:16, 0:W]), [], [A("lw", 0, W)], 4500)
         for c in range(2):
             n = lambda s: "%s%d" % (s, c)
             pa, h = n("pa"), HS[c]
             tag[0] = "F%d" % c
+            cp(A(pa, 257, 256 + 2 * h, 2), H(lf, c), "act")
             energy(c, n("cx"), n("mf"), H("ag", c))
             tag[0] = "T%d" % c
             if c == 1:
                 tt(A("mkc"), A(pa, 128, 192), A("ksc"), AL.is_lt)
                 tt(A(n("mk")), IND(A("mkc"), A("cz")), A("par"), AL.mult)
-                mm(A(pa, 0, h), A(n("mk")), A("prb"), True, True)
+                mm(A(pa, 256, 256 + 2 * h, 2), A(n("mk")), A("prb"), True, True)
             else:
                 tt(A(n("mk"), p=h), A(pa, 128, 256, 1, h), A(n("ks"), p=h), AL.is_lt)
-                mm(A(pa, 0, h), A(n("mk"), p=h), A("ib", 0, h, 1, h), True, True)
-            tt(A(pa, 256, 256 + h), A(pa, 0, h), H("dv", c), AL.mult)
-            tt(A(n("nw")), A(pa, 256, 256 + h), H(lf, c), AL.add)
+                mm(A(pa, 256, 256 + 2 * h, 2), A(n("mk"), p=h), A("ib", 0, h, 1, h), True, True)
+            scan(A(n("n2")), A("dv", 2 * HO[c], 2 * (HO[c] + h)), A(pa, 256, 256 + 2 * h), 0.0, AL.mult, AL.add)
             if t < ST - 1:
                 su = "su%d%d" % (t, c)
-                cp(A(su), A(n("nw")))
+                cp(A(su), A(n("n2"), 1, 2 * h, 2))
                 sends[t, c] = add("pool", "send", (su, "lu%d%d" % (t + 1, c), "arr%d%d" % (t + 1, c)), [], [A(su)],
                                   300, lat=P["SEND"])
             else:
+                cp(A(n("nw")), A(n("n2"), 1, 2 * h, 2))
                 dma("sp", "d_y%d" % c,
                     (lambda cc: lambda T: (T.yl[:, HO[cc]:HO[cc] + HS[cc]], T["nw%d" % cc][:, :]))(c), [], [A(n("nw"))], 2600)
     return ops
@@ -524,25 +542,21 @@ def _deps(ops):
         o["time"] = [x["i"] for x in o["extra"]]
 
 
-def schedule():
-    XL, SL, LOOK = P["XL"], P["SL"], P["LOOK"]
-    ops = build()
-    _deps(ops)
-    n = len(ops)
-    succ = [[] for _ in ops]
-    left = [0] * n
+def _place(ops, succ, p):
+    XL, SL, n = P["XL"], P["SL"], len(ops)
     for o in ops:
-        d = set(o["hard"]) | set(o["soft"]) | set(o["time"])
-        left[o["i"]] = len(d)
-        for j in d:
-            succ[j].append(o["i"])
+        if "gat" in o:
+            t, j, u = o["gat"]
+            o["eng"] = "dve" if p["DG"][t][j] >> u & 1 else "act"
+    left = [len(set(o["hard"]) | set(o["soft"]) | set(o["time"])) for o in ops]
     pr = [0.0] * n
     for i in range(n - 1, -1, -1):
         o = ops[i]
         pr[i] = o["cost"] + max(
             [pr[j] + (0 if i in ops[j]["soft"] else o["lat"] + (SL if o["eng"] == ops[j]["eng"] else XL)) for j in succ[i]]
             + [o["lat"]])
-    pr = [pr[i] + P["BIAS"].get(ops[i]["tag"], 0) + P["FINE"].get(ops[i]["fine"], 0) for i in range(n)]
+    pr = [pr[i] + p["BIAS"].get(o["tag"], 0) + p["FINE"].get(o["fine"], 0) + p["SB"].get(o["st"], 0)
+          for i, o in enumerate(ops)]
     free = dict(dve=0.0, act=0.0, pe=0.0, pool=0.0, sp=0.0)
     free[None] = 0.0
     order = dict((e, []) for e in free if e)
@@ -561,10 +575,9 @@ def schedule():
         if left[i] == 0:
             release(i)
     for _ in range(n):
-        t0, e = min([(max(free[e], min(ready[e].values())), e) for e in ready if ready[e]], key=lambda x: x[0])
-        look = t0 + (LOOK if e in ("dve", "act") else 40)
-        i = max([i for i in ready[e] if ready[e][i] <= look], key=lambda i: (pr[i] - 2 * max(0, ready[e][i] - t0), -i))
-        t = max(t0, ready[e].pop(i))
+        t, e = min([(max(free[e], min(ready[e].values())), e) for e in ready if ready[e]], key=lambda x: x[0])
+        i = max([i for i in ready[e] if ready[e][i] <= t], key=lambda i: (pr[i], -i))
+        ready[e].pop(i)
         o = ops[i]
         o["start"], o["end"] = t, t + o["cost"] + o["lat"]
         if e:
@@ -574,8 +587,65 @@ def schedule():
             left[j] -= 1
             if left[j] == 0:
                 release(j)
-    if P.get("FAST"):
-        return None, order, None, ops
+    return order
+
+
+def _spans(ops, sets):
+    seq = sorted(ops, key=lambda x: (x["start"], x["i"]))
+    q = []
+    for cs, XL, SL, scale in sets:
+        free, end = {}, [0.0] * len(ops)
+        for o in seq:
+            e = o["eng"]
+            t = free.get(e, 0.0) if e else 0.0
+            for j in o["hard"]:
+                t = max(t, end[j] + (SL if ops[j]["eng"] == e else XL))
+            for j in o["time"]:
+                t = max(t, end[j])
+            c, lat = cs[o["i"]]
+            end[o["i"]], free[e] = t + c + lat, t + c
+        q.append(max(end) / scale)
+    return sum(q) / len(q) + max(q), q
+
+
+def schedule():
+    ops = build()
+    _deps(ops)
+    succ = [[] for _ in ops]
+    for o in ops:
+        for j in set(o["hard"]) | set(o["soft"]) | set(o["time"]):
+            succ[j].append(o["i"])
+    sets, keep = [], dict(P)
+    for m, scale in SETS:
+        P.update(m)
+        sets.append(([(o["cost"], o["lat"]) for o in build()], P["XL"], P["SL"], scale))
+        P.update(keep)
+    names = [("BIAS", "tag"), ("FINE", "fine"), ("SB", "st")]
+    names = [(k, sorted(set(o[f] for o in ops))) for k, f in names]
+    z = [12345]
+
+    def rnd(n):
+        z[0] = (z[0] * 1103515245 + 12345) % 2147483648
+        return (z[0] >> 8) % n
+
+    best = dict((k, P[k]) for k in ("BIAS", "FINE", "SB", "DG"))
+    _place(ops, succ, best)
+    score = _spans(ops, sets)
+    for _ in range(P["TRIES"]):
+        p = dict(BIAS=dict(best["BIAS"]), FINE=dict(best["FINE"]), SB=dict(best["SB"]), DG=[list(r) for r in best["DG"]])
+        for _ in range(1 + rnd(2)):
+            u = rnd(4)
+            if u == 3:
+                p["DG"][rnd(ST)][rnd(6)] ^= 1 << rnd(SUB)
+            else:
+                k, ns = names[u]
+                nm = ns[rnd(len(ns))]
+                p[k][nm] = p[k].get(nm, 0) + (2 * rnd(2) - 1) * (500, 2000, 5000, 12000)[rnd(4)]
+        _place(ops, succ, p)
+        s = _spans(ops, sets)
+        if s[0] <= score[0]:
+            best, score = p, s
+    order = _place(ops, succ, best)
     need = set(j for o in ops for j in o["hard"])
     total = {}
     for e in order:
@@ -608,7 +678,7 @@ def schedule():
                     kn[s2] = v2
         o["waits"] = sorted(waits.items())
         o["know"] = dict(kn)
-    return seq, order, total, ops
+    return seq, order, total, ops, score
 
 
 _CACHE = []
@@ -620,7 +690,7 @@ def rank_program(g, core, T, topo):
         return
     if not _CACHE:
         _CACHE.append(schedule())
-    seq, order, total, ops = _CACHE[0]
+    seq, order, total = _CACHE[0][:3]
     n = len(T.cores)
     dst = T.cores[(rank + HOP) % n]
     src = T.cores[(rank - HOP) % n]

from concourse.mybir import AluOpType as AL, ActivationFunctionType as AF

W, S, ST, HOP = 4096, 192, 3, 5
HS, HO = (128, 64), (0, 128)
R = 2
NS = 16 // R
SUB = 4
P = dict(PEF=0.5, GF=1.55, OV=30, XL=220, SL=135, SEND=4500, EQA=(2, 2), EQH=2, AG=[0, 0, 1], TRIES=450,
         EN=['dve', 'act', 'dve', 'dve', 'dve', 'act', 'act'],
         BIAS={'C0': 92000, 'F0': 14900, 'T0': 22800, 'G': 18300, 'D': 23000, 'L': 13400, 'X0': 21800, 'E0': 32300,
               'M0': 4000, 'V0': 89300, 'W0': 20100, 'V1': -800, 'W1': 20600, 'H': 66100, 'K': -400, 'F1': 6000,
               'T1': 53900, 'X1': -3000, 'C1': -32400, 'E1': 40100, 'P0': -11300, 'P1': 37200, 'M1': 8500,
               'U1': -33400, 'U0': -23600, 'Y0': 2300, 'Y1': -20300},
         DG=[[10, 8, 1, 6, 1, 0], [3, 9, 12, 9, 5, 1], [9, 6, 12, 6, 0, 4]],
         FINE={'C1au': -3000, 'P1ks': 8500, 'U0un': -1000, 'F0pa': -4000, 'T0su': 1000, 'Hof': 3000, 'P1tt': -500,
               'E1py': -2000, 'F1mf': 11500, 'Huw': 7000, 'P1pg': 500, 'P1zc': 5500, 'P0tt': 3000, 'M1me': 500,
               'M0ys': 1500, 'F1pa': 7000, 'C0cx': 11500, 'T1su': -1000, 'W1hs': -1500, 'W0ev': 7500, 'W0mh': 4000,
               'C0aa': -1000, 'W1hr': -6500, 'W1pv': 500, 'W1hi': 1500, 'T0pa': 5000, 'Daj': 6000, 'Gsg': -2000,
               'P0ks': -4000, 'P1ms': 6500, 'V0pv': 9000, 'E0pa': -1500, 'T0mk': -1500, 'X1x1': 10000, 'W1vs': 8500,
               'T1nw': 1000, 'Heq': -3500, 'W0zz': 9000, 'P1tl': -1500, 'W0hj': 9500, 'Ht0': -6000, 'Llw': -1500,
               'X0lu': -7500, 'Gpg': -13500, 'Y0l4': 3000, 'T0nw': -9000, 'Gpv': -6000, 'P0pg': -13000, 'C0au': 6000,
               'W1zz': -2500, 'M1ys': 4500, 'W1mh': -2500, 'Hsc': 10000, 'Lsc': -1000, 'W0hr': -6500, 'W0hc': 500,
               'Geq': 7000, 'Y0lf': -6500, 'T1': -12000, 'W0vs': 10000, 'M1pa': -5500, 'P0tl': -3500, 'D': -5500,
               'Dun': -5500, 'C1aa': -1000, 'Ht2': -7000, 'Lof': 2500, 'W1ev': -7000, 'T1mk': -1500, 'Y1l4': -5500,
               'W0hs': -4500, 'W0pv': -4500, 'Dai': -6500, 'T1pa': 6500, 'P1pa': 15000, 'W0ac': -5000, 'Gpd': -5500,
               'X0x0': 5500, 'M0me': -500, 'T0': -2000, 'P1pu': 3500, 'W1pd': 2000, 'F0mf': 9500, 'T0n2': -4500,
               'E0py': 6500, 'W0ab': 9500, 'Gag': 9500, 'Y1lf': -5000, 'P0pa': -500, 'Lt4': -5500, 'T1n2': -5500,
               'U1un': -4500, 'P0pu': 5500, 'V1pv': 4000, 'E1pa': 2000, 'U1py': 9000, 'W1ac': -500, 'P0ms': 1500,
               'V0v0': 2500, 'W1ab': -5500, 'V1v1': 2000},
         SB={'La': -44000, 'Hb': 2000, 'T0c': 16000, 'E0c': -8000, 'E1a': -24000, 'U1b': 16000, 'T0a': 4000, 'Ga': 15000,
             'P1b': -13000, 'W1b': 8000, 'C0a': 9000, 'P1a': -3000, 'C0c': 7000, 'X1c': -8000, 'X0a': -5000, 'U0a': 11000,
             'W1a': 4000, 'Ha': -2000, 'C0b': -16000, 'M1c': 1000, 'Gb': 2000, 'V0c': -3000, 'E0b': 18000, 'V0b': 13000,
             'T1a': -2000, 'Hc': 4000, 'U1c': -1000, 'V1a': 6000, 'T0b': 5000, 'E1c': 12000, 'P1c': 10000, 'X1b': 4000,
             'U0b': -7000, 'F0b': 1000, 'F1c': -2000, 'Lb': -15000, 'E0a': -12000, 'C1a': -8000, 'T1b': 8000,
             'X0c': -8000, 'M0b': -5000, 'V0a': 21000, 'V1b': 12000, 'Y1c': -23000, 'X1a': -4000, 'Db': -4000,
             'E1b': 12000, 'Y0a': -4000, 'W0c': -1000, 'F0a': 8000, 'Y0b': 1000, 'M1a': 1000, 'M1b': 12000, 'W0b': 12000,
             'M0a': 3000, 'X0b': 8000, 'Y1b': -23000, 'U0c': 13000, 'W0a': 8000, 'P0b': 4000, 'Dc': -28000, 'V1c': 4000,
             'C1b': -4000, 'Da': 16000, 'Lc': -1000, 'F1a': 1000})
SETS = [(dict(XL=250, SL=150, SEND=4500), 105500), (dict(GF=2.0, XL=175, SL=105, SEND=3300), 107000),
        (dict(GF=1.2, XL=210, SL=130, SEND=5000, PEF=0.55), 103000)]
MAGIC = 12582912.0
F, B, I, U = "float32", "bfloat16", "int32", "uint16"

SCRATCH = {}
BUF = {}
POOLED = ("pci pki pgi p1i p2i sa sa2 sbi sb2 jgi c15i czi saf sbf rw i32f j192 j4096 half zero wrow wtmp wsc thd seg0 "
          "rst idf bof bom ib i16 bob kc kh i192 ibig ones qg qk im16 wbig diag cy nthd nthr pick pik2 pik5 kcc kci prf "
          "prb par q2 q8 ibc").split()


def _sb(name, n, dt, where="sbuf"):
    if name in POOLED:
        pool = "pool_" + dt
        at = SCRATCH[pool][1][1] if pool in SCRATCH else 0
        SCRATCH[pool] = ("sbuf", [128, at + (n + 15) // 16 * 16], dt)
        BUF[name] = (where, [128, n], dt, pool, at)
    else:
        SCRATCH[name] = (where, [128, n], dt)
        BUF[name] = (where, [128, n], dt, name, 0)


for _n, _w, _d in [
    ("xw", 2 * W, B), ("nbw", W, I), ("lw", W + S, F), ("tri", S, I), ("lbi", 256, I), ("lbb", 256, F), ("jrf", S, F),
    ("thi", 4, I), ("jrow", S, B), ("pci", 4, I), ("pki", 4, I), ("pgi", 4, I), ("p1i", 4, I), ("p2i", 4, I),
    ("cols", 24, F), ("qg", 128, B), ("qk", S, B), ("q2", 128, B), ("q8", 64, B), ("kci", 64, B), ("kcc", 64, B),
    ("prf", 64, F), ("prb", 64, B), ("par", 128, B), ("ibc", 64, B), ("czi", 8, I), ("cz", 8, U),
    ("ib", 128, B), ("idf", 128, F), ("bob", 128, B), ("bof", 128, F), ("bom", 128, F), ("i32f", 8, F), ("im16", 8, B),
    ("wbig", 144, B), ("pm_s", 1024, B), ("dm_s", 1024, B), ("rm_s", 1024, B), ("sa", 8, I), ("sa2", 8, I), ("saf", 8, F),
    ("sbi", 8, I), ("sb2", 8, I), ("sbf", 8, F), ("rw", 8, F), ("kc", 128, B), ("kh", 128, B), ("i192", 128, B),
    ("ibig", 128, B), ("ones", 128, B), ("diag", S, B), ("seg0", S, F), ("rst", 128, F), ("jgi", 12, I),
    ("j192", 24, F), ("j4096", 24, F), ("half", S, F), ("zero", S, F), ("wrow", S, F), ("thd", S, F),
    ("wtmp", S, F), ("wsc", S, F), ("c15i", 8, I), ("c15", 8, U), ("i16", 128, B), ("cy", 128, B), ("nthd", S, B),
    ("nthr", S, B), ("sg", S, B), ("pick", S, F), ("pik2", S, F), ("pik5", S, F),
    ("lf0", S, F), ("lf1", S, F), ("l4", S, F), ("unb", S, F), ("uw", 2 * S, F), ("pu", S, U), ("pgs", S, F),
    ("pgu", 12, U), ("pgf", 24, F), ("hi", S, I), ("hj", S, I), ("hrs", S, B), ("hsc", S, F), ("hc", 12, F),
    ("eqh", 1248, B), ("eqd", 704, F), ("nwc", 12, F), ("eqp", 1248, B), ("sc", S, F), ("t0", 24, F), ("t2", 24, F),
    ("offu", 12, U), ("ag", S, B), ("agd", 128, B), ("scp", S, F), ("t4", 24, F),
    ("ofp", 12, U), ("un", S, F), ("ai", S, I), ("aj", S, I), ("dv", 2 * S, F), ("ksc", 64, F), ("zc", 128, F),
    ("mkc", 64, B),
]:
    _sb(_n, _w, _d)
for _c in range(2):
    _h = HS[_c]
    for _n, _w, _d in [("x", 16 * _h, B), ("cx", 16 * _h, B), ("v", 16 * _h, B), ("me", 16 * _h, F), ("mf", 16 * _h, F),
                       ("ys", _h, F), ("ac", 4 * _h, B), ("ks", 128, F), ("ms", 128, F), ("tt", 128, B), ("tl", _h, F),
                       ("ab", 4 * _h, B), ("vs", _h, B), ("ev", 9 * _h, B), ("mh", 128, F), ("zz", 128, F),
                       ("aa", _h, F), ("au", _h, U), ("mk", 128, B), ("nw", _h, F), ("n2", 2 * _h, F)]:
        _sb("%s%d" % (_n, _c), _w, _d)
    for _t in range(ST):
        _sb("lu%d%d" % (_t, _c), _h, U)
    for _t in range(ST - 1):
        _sb("su%d%d" % (_t, _c), _h, U)
for _n in ("py0", "py1", "pa0", "pa1", "pv0", "pv1", "pd0", "pd1"):
    _sb(_n, 512, F, "psum")

DMAS = ["d_tr", "d_lb", "d_th", "d_xs", "d_lw", "d_nb", "d_x2", "d_y0", "d_y1", "d_yb"]
ARRS = ["arr%d%d" % (t, c) for t in range(1, ST) for c in range(2)]
SEMAPHORES = ["s_dve", "s_act", "s_pe", "s_pool", "sent"] + DMAS + ARRS


def A(name, c0=0, c1=None, st=1, p=128):
    return (name, p, c0, BUF[name][1][1] if c1 is None else c1, st)


def IND(win, off):
    return ("#", win, off)


def _n(a):
    return 16 * _n(a[2]) if a[0] == "#" else len(range(a[2], a[3], a[4]))


def _ap(T, a):
    if not isinstance(a, tuple):
        return a
    if a[0] == "#":
        return _ap(T, a[1]).indirect(_ap(T, a[2]))
    buf, at = BUF[a[0]][3:]
    if a[4] == 1:
        return T[buf][0:a[1], at + a[2]:at + a[3]]
    return T[buf][0:a[1], at + a[2]:at + a[3]:a[4]]


def _ps(a):
    return a[0] != "#" and BUF[a[0]][0] == "psum"


def _two(a):
    return BUF[a[0]][2] in (B, U)


def build():
    ops = []
    OV = P["OV"]
    tag = ["K", ""]

    def add(eng, kind, args, outs, ins, cost, **kw):
        rd, wr = [], []
        for a in ins:
            if isinstance(a, tuple):
                rd += [a[1], a[2]] if a[0] == "#" else [a]
        for a in outs:
            if a[0] == "#":
                wr.append(a[1])
                rd.append(a[2])
            else:
                wr.append(a)
        o = dict(tag=tag[0], eng=eng, kind=kind, args=args, rd=rd, wr=wr, cost=cost, extra=[], lat=0)
        o["st"] = tag[0] + tag[1]
        o["fine"] = tag[0] + (wr[0][0][:2] if wr else "")
        o.update(kw)
        ops.append(o)
        return o

    def vcost(out, ins, base):
        n = _n(out)
        if out[0] == "#":
            return 70 + 3.5 * n
        if ins[0][0] == "#":
            return 70 + P["GF"] * n
        return OV + max(64, base * n)

    def cp(out, a, eng="dve"):
        half = eng == "dve" and out[0] != "#" and a[0] != "#" and _two(out) and _two(a)
        return add(eng, "cp", (out, a), [out], [a], vcost(out, [a], 0.5 if half else 1))

    def ts(out, a, s1, s2, o0, o1=None):
        return add("dve", "ts", (out, a, s1, s2, o0, o1), [out], [a, s1, s2],
                   vcost(out, [a], 0.5 if _two(out) and _two(a) else 1))

    def tt(out, a, b, op):
        return add("dve", "tt", (out, a, b, op), [out], [a, b], vcost(out, [a], 1 if _ps(a) or _ps(b) else 2))

    def scan(out, d0, d1, init, o0, o1):
        return add("dve", "scan", (out, d0, d1, init, o0, o1), [out], [d0, d1], vcost(out, [d0], 1))

    def ms(out, val):
        return add("dve", "ms", (out, val), [out], [], OV + max(64, _n(out) * (0.5 if _two(out) else 1)))

    def act(out, a, fn, bias, scale=1.0):
        return add("act", "act", (out, a, fn, bias, scale), [out], [a, bias, scale], vcost(out, [a], 1))

    def scaled(out, a, s):
        return act(A(out), A(a), AF.Identity, 0.0, s)

    def mm(out, l, r, st, sp):
        c = max(min(64, _n(l)), _n(r)) * (4 if BUF[l[0]][2] == F else 1) * P["PEF"] + 4
        return add("pe", "mm", (out, l, r, st, sp), [out], [l, r], c)

    def iota(out, pat, base, cm):
        return add("pool", "iota", (out, pat, base, cm), [out], [], 160 + 2 * _n(out))

    def dma(q, sem, fn, outs, ins, lat):
        return add(q, "dma", fn, outs, ins, 60, sem=sem, lat=lat)

    col = lambda j, p=128: A("cols", j, j + 1, 1, p)
    PF, PK, PG, P16, M0, KM, KH, TH, G16, C1, C4096, PK4, PK2, PK5, PK6, P1, PH, KP, MB, P7, C2, C512 = range(22)

    ms(A("lw", 0, 536), 0.0)
    for u in range(1, 8):
        cp(A("lw", 536 * u, 536 * u + 536), A("lw", 0, 536), "act")
    ld = [dma("sp", "d_tr", lambda T: (T.tri[:, :], T.tr[:, :]), [A("tri")], [], 2400),
          dma("sp", "d_lb", lambda T: (T.lbi[:, :], T.lb[:, :]), [A("lbi")], [], 2400),
          dma("sp", "d_xs", lambda T: (T.xw[:, 0:W], T.xs[:, :]), [A("xw", 0, W)], [], 6500),
          dma("sp", "d_th", lambda T: (T.thi[:, 0:1], T.th[:, :]), [A("thi", 0, 1)], [], 6500)]
    cp(A("lbb"), A("lbi"))
    ld += [dma("sp", "d_lw", lambda T: (T.lw[0:128:16, 0:W], T.lbb[:, :]), [A("lw", 0, W)], [A("lbb")], 4000),
           dma("sp", "d_nb", lambda T: (T.nbw[:, :], T.nb[:, :]), [A("nbw")], [], 9000),
           dma("sp", "d_x2", lambda T: (T.xw[:, W:2 * W], T.xs[:, :]), [A("xw", W, 2 * W)], [], 12000)]
    for a, b in zip(ld, ld[1:]):
        b["after"] = a

    iota(A("pci", 0, 1), [[0, 1]], 0, 1)
    iota(A("jrow"), [[1, S]], 0, 0)
    iota(A("qg"), [[1, 8], [0, 16]], 0, 0)
    iota(A("qk"), [[0, 12], [1, 16]], 0, 0)
    iota(A("c15i"), [[16, 8]], 15, 0)
    iota(A("sa"), [[-1, 8]], 15, 1)
    iota(A("sbi"), [[1, 8]], 1, 1)
    iota(A("jgi"), [[16, 12]], 0, 0)
    pc, pk = A("pci", 0, 1), A("pki", 0, 1)
    ts(pk, pc, 15, None, AL.bitwise_and)
    ts(A("pgi", 0, 1), pc, 4, None, AL.arith_shift_right)
    cp(col(PF), pc)
    cp(col(PK), pk)
    cp(col(PG), A("pgi", 0, 1))
    ts(col(P16), pc, 16.0, None, AL.add)
    ts(col(M0), pk, 0.0, None, AL.is_equal)
    ts(col(KM), pk, -15.0, None, AL.add)
    ts(col(KH), pk, -512.0, 7680.0, AL.mult, AL.add)
    ts(col(TH), A("thi", 0, 1), -16.0, -0.5, AL.mult, AL.add)
    ts(col(G16), A("pgi", 0, 1), 16.0, None, AL.mult)
    ts(col(PK4), pk, 4096.0, -61440.0, AL.mult, AL.add)
    ts(col(PK2), pk, 2.0, -30.0, AL.mult, AL.add)
    ts(col(PK5), pk, 512.0, -7680.0, AL.mult, AL.add)
    ts(col(PK6), pk, 512.0, -7488.0, AL.mult, AL.add)
    ms(col(C1), 1.0)
    ms(col(C2), 2.0)
    ms(col(C512), 512.0)
    ms(col(C4096), 4096.0)
    j128 = A("jrow", 0, 128)
    ts(A("ib"), j128, col(PF), None, AL.is_equal)
    scaled("i16", "ib", 0.0625)
    ms(A("cy"), -0.46875)
    scaled("idf", "ib", 1.0)
    scaled("kc", "ib", col(KM))
    scaled("kh", "ib", col(KH))
    scaled("i192", "ib", 192.0)
    scaled("ibig", "ib", -float(2 ** 26))
    ts(A("bob"), A("qg"), col(PG), None, AL.is_equal)
    scaled("bof", "bob", 1.0)
    scaled("bom", "bob", -16.0)
    ts(A("i32f"), A("jrow", 0, 8), col(PG), 32.0, AL.is_equal, AL.mult)
    ts(A("im16"), A("jrow", 0, 8), col(PG), -16.0, AL.is_equal, AL.mult)
    ts(A("wbig"), A("jrow", 0, 144), col(P16), col(M0), AL.is_equal, AL.mult)
    ts(A("sa2"), A("sa"), 15, None, AL.bitwise_and)
    ts(A("saf"), A("sa2"), col(G16), None, AL.add)
    ts(A("sb2"), A("sbi"), 15, None, AL.bitwise_and)
    ts(A("sbf"), A("sb2"), col(PK), col(G16), AL.min, AL.add)
    ms(A("rw", 0, 7), 8192.0)
    ts(A("rw", 7, 8), pk, 8.0, 8192.0, AL.is_lt, AL.mult)
    for s in range(8):
        ts(A("pm_s", 128 * s, 128 * s + 128), j128, A("saf", s, s + 1), -1.0, AL.is_equal, AL.mult)
        d = A("pd%d" % (s // 4), 128 * (s % 4), 128 * (s % 4 + 1))
        mm(d, A("ib"), A("ib"), True, False)
        mm(d, A("ib"), A("pm_s", 128 * s, 128 * s + 128), False, True)
        ts(A("rm_s", 128 * s, 128 * s + 128), j128, A("sbf", s, s + 1), A("rw", s, s + 1), AL.is_equal, AL.mult)
    for s in range(2):
        cp(A("dm_s", 512 * s, 512 * s + 512), A("pd%d" % s), "act")
    ms(A("ones"), 1.0)
    ts(A("diag"), A("qk"), col(PK), None, AL.is_equal)
    for n, step in (("pick", C4096), ("pik2", C2), ("pik5", C512)):
        act(A(n), A("diag"), AF.Identity, col(step), -float(2 ** 20))
    ts(A("seg0"), A("qk"), 0.0, None, AL.not_equal)
    ts(A("rst"), A("qk", 0, 128), 0.0, float(2 ** 25), AL.is_equal, AL.mult)
    for n, base in (("j192", 192.0), ("j4096", 4096.0)):
        ms(A(n, 0, 24, 2), -65536.0)
        ts(A(n, 1, 24, 2), A("jgi"), col(PK), base, AL.add, AL.add)
    ms(A("half"), 0.5)
    ms(A("zero"), 0.0)
    scan(A("wrow"), A("half"), A("zero"), float(2 ** 96), AL.mult, AL.add)
    scaled("nthr", "wrow", -2.5)
    ts(A("thd"), A("qk"), col(PK), -float(2 ** 98), AL.not_equal, AL.mult)
    tt(A("nthd"), A("thd"), A("nthr"), AL.add)
    tt(A("wtmp"), A("wrow"), A("diag"), AL.mult)
    scan(A("wsc"), A("seg0"), A("wtmp"), 0.0, AL.mult, AL.max)
    ts(A("nwc"), A("wsc", 15, S, 16), -1.0, None, AL.mult)
    cp(A("jrf"), A("jrow"), "act")
    cp(A("c15"), A("c15i"))
    cp(A("uw", S, 2 * S), A("zero"), "act")
    cp(A("dv", 0, 2 * S, 2), A("zero"), "act")
    for n in ("ks1", "ms1", "mh1"):
        cp(A(n), A("zero", 0, 128), "act")
    iota(A("q2"), [[0, 8], [1, 2], [0, 8]], 0, 0)
    iota(A("q8"), [[1, 8], [0, 8]], 0, 0)
    iota(A("kci"), [[0, 8], [1, 8]], 0, 0)
    iota(A("czi"), [[8, 8]], 0, 0)
    ts(A("p1i", 0, 1), pc, 1, None, AL.bitwise_and)
    ts(A("p1i", 1, 2), pc, 7, None, AL.bitwise_and)
    ts(A("p2i", 0, 1), pc, 1, None, AL.arith_shift_right)
    cp(col(P1), A("p1i", 0, 1))
    cp(col(PH), A("p2i", 0, 1))
    cp(col(P7), A("p1i", 1, 2))
    ts(col(KP), A("p1i", 0, 1), 8.0, -15.0, AL.mult, AL.add)
    ts(col(MB), pk, 0.0, -float(2 ** 26), AL.is_equal, AL.mult)
    ts(A("kcc"), A("kci"), col(KP), None, AL.add)
    ts(A("prb"), A("jrow", 0, 64), col(PH), None, AL.is_equal)
    scaled("prf", "prb", 1.0)
    ts(A("par"), A("q2"), col(P1), None, AL.is_equal)
    ts(A("ibc"), A("q8"), col(PG), col(MB), AL.is_equal, AL.mult)
    ts(A("cz"), A("czi"), col(P7), None, AL.add)

    def gather(dst, win, off, t, j):
        q = HS[j % 2] // SUB
        for u in range(SUB):
            cp(A(dst, 16 * q * u, 16 * q * (u + 1)), IND(win, A(off, q * u, q * (u + 1))), "act")["gat"] = (t, j, u)

    def energy(c, x, m, last):
        pa, py, h = "pa%d" % c, "py%d" % c, HS[c]
        n = h * R
        if c == 1:
            mm(A(pa, 128, 192), A("ib"), A("kcc"), True, False)
            for i in range(8):
                mm(A(pa, 128 + i, 192, 8), A(x, i, None, 8), A("im16"), False, False)
            for i in range(8):
                tt(A(m, i * n, (i + 1) * n), A(x, i, None, 8), A(py, 0, n), AL.max)
                mm(A(pa, 128 + i, 192, 8), A(m, i * n, (i + 1) * n), A("i32f"), False, last is None and i == 7)
            if last is not None:
                mm(A(pa, 128, 192), A("agd"), A("ibc"), False, True)
            return
        mm(A(pa, 128, 256, 1, h), A("ones", 0, h), A("kc"), True, False)
        for k in range(16):
            mm(A(pa, 128 + k, 256, 16, h), A(x, k, None, 16), A("im16"), False, False)
        for i in range(NS):
            tt(A(m, i * n, (i + 1) * n), A(x, i, None, NS), A(py, 0, n), AL.max)
            for a in range(R):
                end = last is None and i == NS - 1 and a == R - 1
                mm(A(pa, 128 + NS * a + i, 256, 16, h), A(m, i * n + a, (i + 1) * n, R), A("i32f"), False, end)
        if last is not None:
            mm(A(pa, 128, 256, 1, h), last, A("ibig"), False, True)

    def firsts(eq, row, scal, bank, less, on_act):
        o = 0
        mm(A(bank, 256, 448), A("ib"), A(less), True, False)
        for hh in range(12):
            n = S - 16 * hh
            w = A("wsc", 16 * hh + 15, 16 * hh + 16)
            if hh < on_act:
                act(A("eqd", o, o + n), A(row, 16 * hh, S), AF.Abs, scal(hh), -1.0)
                act(A(eq, o, o + n), A("eqd", o, o + n), AF.Relu, w, A("nwc", hh, hh + 1))
            else:
                ts(A(eq, o, o + n), A(row, 16 * hh, S), scal(hh), w, AL.is_equal, AL.mult)
            mm(A(bank, 256 + 16 * hh, 448), A("bob"), A(eq, o, o + n), False, hh == 11)
            o += n

    H = lambda name, c: A(name, HO[c], HO[c] + HS[c])
    G = lambda name, c: A(name, HO[c] // 16, (HO[c] + HS[c]) // 16)
    E15 = lambda name, c: A(name, HO[c] + 15, HO[c] + HS[c], 16)
    sends = {}
    for t in range(ST):
        lf = "lf%d" % (t % 2)
        tag[1] = "abc"[t]
        for c in range(2):
            lu = "lu%d%d" % (t, c)
            tag[0] = "X%d" % c
            if t == 0:
                cp(A(lu), H("tri", c))
            else:
                add(None, "recv", None, [A(lu)], [], 0, sem="arr%d%d" % (t, c), extra=[sends[t - 1, c]])
            gather("x%d" % c, A("xw", 0, W), lu, t, c)
            tag[0] = "Y%d" % c
            cp(H(lf, c), A(lu))
            act(H("l4", c), H(lf, c), AF.Identity, col(C4096))
        cp(A("uw", 0, S), A("zero"), "act")
        for c in range(2):
            n = lambda s: "%s%d" % (s, c)
            pa, py, h = n("pa"), n("py"), HS[c]
            tag[0] = "E%d" % c
            mm(A(pa, 0, h), A("ib"), A("cy", 0, h), True, False)
            for k in range(16):
                mm(A(pa, 0, h), A("i16"), A(n("x"), k, None, 16), False, k == 15)
            for i in range(R):
                ts(A(py, i, h * R, R), A(pa, 0, h), MAGIC, -MAGIC, AL.add, AL.add)
            tag[0] = "M%d" % c
            energy(c, n("x"), n("me"), None)
            cp(A(n("ys")), A(py, 0, h * R, R), "act")
            tag[0] = "P%d" % c
            et = A(pa, 128, 256, 1, h)
            kl, kr = A(n("ks"), p=h), A("idf", 0, h, 1, h)
            if c == 1:
                cp(A("ksc"), A(pa, 128, 192), P["EN"][6])
                tt(A("zc"), IND(A("ksc"), A("cz")), A("par"), AL.mult)
                et = A(pa, 256, 384, 1, h)
                mm(et, A("prf"), A("zc"), True, True)
                kl, kr = A("zc"), A("prf")
            scan(A(n("ms"), p=h), A("rst", p=h), et, 0.0, AL.add, AL.min)
            cp(A(n("ks"), p=h), et, P["EN"][c])
            tt(A(n("tt")), IND(A(n("ms")), A("c15")), A(n("ks")), AL.is_equal)
            mm(A(pa, 0, h), A(n("tt"), p=h), A("ib", 0, h, 1, h), True, True)
            tag[0] = "U%d" % c
            mm(A(py, 256, 256 + h), A("bom"), A(n("ys")), True, False)
            mm(A(py, 256, 256 + h), kl, kr, False, True)
            act(H("unb", c), A(py, 256, 256 + h), AF.Sign, col(TH))
            tag[0] = "P%d" % c
            tt(A(n("tl")), A(pa, 0, h), H(lf, c), AL.mult)
            mm(A(pa, 0, h), A("bof"), A(n("tl")), True, True)
            scan(H("pgs", c), A("pick", 0, h), A(pa, 0, h), 0.0, AL.add, AL.max)
            cp(H("pu", c), A(pa, 0, h))
            ts(G("pgu", c), E15("pgs", c), col(PK4), None, AL.add)
        for c in range(2):
            n = lambda s: "%s%d" % (s, c)
            pv, h = n("pv"), HS[c]
            tag[0] = "V%d" % c
            gather(n("v"), A("lw", 0, W), "lu%d%d" % (t, c), t, 2 + c)
            for k in range(16):
                mm(A(pv, 0, h), A("wbig", 16 - k, 144 - k), A(n("v"), k, None, 16), k == 0, k == 15)
            tag[0] = "W%d" % c
            cp(A(n("vs")), A(pv, 0, h), P["EN"][2 + c])
            tt(A(n("ev"), 8 * h, 9 * h), A(pv, 0, h), H("jrow", c), AL.is_equal)
            for s in range(8):
                mm(A("pd%d" % (s // 4), h * (s % 4), h * (s % 4 + 1)), A("dm_s", 128 * s, 128 * s + 128), A(n("vs")), True, True)
            kt = A(pv, 128, 256, 1, h)
            mm(kt, A("ones", 0, h), A("kh"), True, False)
            mm(kt, A(n("vs")), A("ib"), False, False)
            mm(kt, A(n("ev"), 8 * h, 9 * h), A("i192"), False, False)
            for b, tmp in ((0, "ac"), (1, "ab")):
                e, d = A(n("ev"), 4 * h * b, 4 * h * (b + 1)), A("pd%d" % b, 0, 4 * h)
                if P["EQA"][c] > 1 - b:
                    act(A(n(tmp)), d, AF.Abs, 0.0)
                    act(e, A(n(tmp)), AF.Relu, col(C1), -1.0)
                else:
                    ts(e, d, 0.0, None, AL.is_equal)
            for s in range(8):
                mm(kt, A(n("ev"), h * s, h * s + h), A("rm_s", 128 * s, 128 * s + 128), False, s == 7)
            scan(A(n("mh"), p=h), A("seg0", 0, 128, 1, h), kt, 0.0, AL.mult, AL.max)
            cp(A(n("zz")), IND(A(n("mh")), A("c15")), P["EN"][4 + c])
            mm(A(pv, 256, 256 + h), A(n("zz"), p=h), A("idf", 0, h, 1, h), True, True)
            cp(H("hi", c), A(pv, 256, 256 + h))
            ts(H("hj", c), H("hi", c), 511, None, AL.bitwise_and)
            ts(H("hrs", c), H("hj", c), -192.0, None, AL.add)
            scan(H("hsc", c), A("pik5", 0, h), H("hrs", c), 0.0, AL.add, AL.max)
            ts(G("hc", c), E15("hsc", c), col(PK5), None, AL.add)
        tag[0] = "H"
        ts(A("t0", 1, 24, 2), A("hsc", 15, S, 16), col(PK6), None, AL.add)
        firsts("eqh", "hrs", lambda hh: A("hc", hh, hh + 1), "pv0", "nthd", P["EQH"])
        scan(A("sc"), A("seg0"), A("pv0", 256, 448), 0.0, AL.mult, AL.max)
        ts(A("t0", 0, 24, 2), A("sc", 15, S, 16), 0.0, 1024.0, AL.is_gt, AL.mult)
        scan(A("t2"), A("j192"), A("t0"), 0.0, AL.min, AL.max)
        cp(A("offu"), A("t2", 1, 24, 2))
        tt(IND(A("uw"), A("offu")), A("unb"), A("l4"), AL.mult)
        for c in range(2):
            tag[0] = "C%d" % c
            tt(A("aa%d" % c), IND(A("nbw"), G("pgu", c)), H("uw", c), AL.max)
            cp(A("au%d" % c), A("aa%d" % c))
            gather("cx%d" % c, A("xw"), "au%d" % c, t, 4 + c)
        tag[0] = "G"
        ts(A("pgf", 1, 24, 2), A("pgs", 15, S, 16), col(PK4), None, AL.add)
        firsts("eqp", "pu", lambda hh: A("pgf", 2 * hh + 1, 2 * hh + 2), "pv1", "nthr", 0)
        cp(A("pd0", S, 2 * S), A(lf), "act")
        if P["AG"][t]:
            ts(A("pd0", 0, S), A("pv1", 256, 448), 0.0, None, AL.is_lt)
            ts(A("ag"), A("pv1", 256, 448), 0.0, None, AL.is_gt)
        else:
            act(A("sg"), A("pv1", 256, 448), AF.Sign, 0.0)
            act(A("pd0", 0, S), A("sg"), AF.Relu, 0.0, -1.0)
            act(A("ag"), A("sg"), AF.Relu, 0.0)
        for a in range(2):
            cp(A("agd", a, 128, 2), H("ag", 1), "act")
        tag[0] = "L"
        scan(A("scp"), A("pik2"), A("ag"), 0.0, AL.add, AL.max)
        ts(A("pgf", 0, 24, 2), A("scp", 15, S, 16), col(PK2), 8192.0, AL.add, AL.mult)
        scan(A("t4"), A("j4096"), A("pgf"), 0.0, AL.min, AL.max)
        cp(A("ofp"), A("t4", 1, 24, 2))
        cp(IND(A("lw"), A("ofp")), A("jrf"))
        tag[0] = "D"
        tt(A("un"), A("uw", 0, S), A("pd0", 0, S), AL.mult)
        tt(A("ai"), IND(A("nbw"), A("pgu")), A("un"), AL.max)
        ts(A("aj"), A("ai"), 4095, None, AL.bitwise_and)
        tt(A("dv", 1, 2 * S, 2), A("aj"), A("pd0", S, 2 * S), AL.subtract)
        if t == ST - 1:
            dma("sp", "d_yb", lambda T: (T.yb[:, :], T.lw[0:128:16, 0:W]), [], [A("lw", 0, W)], 4500)
        for c in range(2):
            n = lambda s: "%s%d" % (s, c)
            pa, h = n("pa"), HS[c]
            tag[0] = "F%d" % c
            cp(A(pa, 257, 256 + 2 * h, 2), H(lf, c), "act")
            energy(c, n("cx"), n("mf"), H("ag", c))
            tag[0] = "T%d" % c
            if c == 1:
                tt(A("mkc"), A(pa, 128, 192), A("ksc"), AL.is_lt)
                tt(A(n("mk")), IND(A("mkc"), A("cz")), A("par"), AL.mult)
                mm(A(pa, 256, 256 + 2 * h, 2), A(n("mk")), A("prb"), True, True)
            else:
                tt(A(n("mk"), p=h), A(pa, 128, 256, 1, h), A(n("ks"), p=h), AL.is_lt)
                mm(A(pa, 256, 256 + 2 * h, 2), A(n("mk"), p=h), A("ib", 0, h, 1, h), True, True)
            scan(A(n("n2")), A("dv", 2 * HO[c], 2 * (HO[c] + h)), A(pa, 256, 256 + 2 * h), 0.0, AL.mult, AL.add)
            if t < ST - 1:
                su = "su%d%d" % (t, c)
                cp(A(su), A(n("n2"), 1, 2 * h, 2))
                sends[t, c] = add("pool", "send", (su, "lu%d%d" % (t + 1, c), "arr%d%d" % (t + 1, c)), [], [A(su)],
                                  300, lat=P["SEND"])
            else:
                cp(A(n("nw")), A(n("n2"), 1, 2 * h, 2))
                dma("sp", "d_y%d" % c,
                    (lambda cc: lambda T: (T.yl[:, HO[cc]:HO[cc] + HS[cc]], T["nw%d" % cc][:, :]))(c), [], [A(n("nw"))], 2600)
    return ops


def _deps(ops):
    hist, bank = {}, {}
    for i, o in enumerate(ops):
        o["i"] = i
        hard, soft = set(), set()
        for a, w in [(a, False) for a in o["rd"]] + [(a, True) for a in o["wr"]]:
            cs = frozenset(range(a[2], a[3], a[4]))
            keep = []
            for (j, cj, wj) in hist.get(a[0], []):
                hit = (w or wj) and j != i and not cs.isdisjoint(cj)
                if hit:
                    if o["kind"] == "mm" and ops[j]["kind"] == "mm":
                        soft.add(j)
                    else:
                        hard.add(j)
                if not (w and hit and cj <= cs and o["kind"] != "mm"):
                    keep.append((j, cj, wj))
            keep.append((i, cs, w))
            hist[a[0]] = keep
            if _ps(a):
                e = o["eng"]
                st = bank.setdefault(a[0], dict(e=e, cur=[], prev=[]))
                if st["e"] != e:
                    st["prev"], st["cur"], st["e"] = st["cur"], [], e
                hard.update(st["prev"])
                if e == "pe" and st["cur"]:
                    soft.add(st["cur"][-1])
                if i not in st["cur"]:
                    st["cur"].append(i)
        if "after" in o:
            soft.add(o["after"]["i"])
        o["hard"] = sorted(hard)
        o["soft"] = sorted(soft - hard)
        o["time"] = [x["i"] for x in o["extra"]]


def _place(ops, succ, p):
    XL, SL, n = P["XL"], P["SL"], len(ops)
    for o in ops:
        if "gat" in o:
            t, j, u = o["gat"]
            o["eng"] = "dve" if p["DG"][t][j] >> u & 1 else "act"
    left = [len(set(o["hard"]) | set(o["soft"]) | set(o["time"])) for o in ops]
    pr = [0.0] * n
    for i in range(n - 1, -1, -1):
        o = ops[i]
        pr[i] = o["cost"] + max(
            [pr[j] + (0 if i in ops[j]["soft"] else o["lat"] + (SL if o["eng"] == ops[j]["eng"] else XL)) for j in succ[i]]
            + [o["lat"]])
    pr = [pr[i] + p["BIAS"].get(o["tag"], 0) + p["FINE"].get(o["fine"], 0) + p["SB"].get(o["st"], 0)
          for i, o in enumerate(ops)]
    free = dict(dve=0.0, act=0.0, pe=0.0, pool=0.0, sp=0.0)
    free[None] = 0.0
    order = dict((e, []) for e in free if e)
    ready = dict((e, {}) for e in free)

    def release(i):
        o = ops[i]
        r = 0.0
        for j in o["hard"]:
            r = max(r, ops[j]["end"] + (SL if ops[j]["eng"] == o["eng"] else XL))
        for j in o["time"]:
            r = max(r, ops[j]["end"])
        ready[o["eng"]][i] = r

    for i in range(n):
        if left[i] == 0:
            release(i)
    for _ in range(n):
        t, e = min([(max(free[e], min(ready[e].values())), e) for e in ready if ready[e]], key=lambda x: x[0])
        i = max([i for i in ready[e] if ready[e][i] <= t], key=lambda i: (pr[i], -i))
        ready[e].pop(i)
        o = ops[i]
        o["start"], o["end"] = t, t + o["cost"] + o["lat"]
        if e:
            free[e] = t + o["cost"]
            order[e].append(i)
        for j in succ[i]:
            left[j] -= 1
            if left[j] == 0:
                release(j)
    return order


def _spans(ops, sets):
    seq = sorted(ops, key=lambda x: (x["start"], x["i"]))
    q = []
    for cs, XL, SL, scale in sets:
        free, end = {}, [0.0] * len(ops)
        for o in seq:
            e = o["eng"]
            t = free.get(e, 0.0) if e else 0.0
            for j in o["hard"]:
                t = max(t, end[j] + (SL if ops[j]["eng"] == e else XL))
            for j in o["time"]:
                t = max(t, end[j])
            c, lat = cs[o["i"]]
            end[o["i"]], free[e] = t + c + lat, t + c
        q.append(max(end) / scale)
    return sum(q) / len(q) + max(q), q


def schedule():
    ops = build()
    _deps(ops)
    succ = [[] for _ in ops]
    for o in ops:
        for j in set(o["hard"]) | set(o["soft"]) | set(o["time"]):
            succ[j].append(o["i"])
    sets, keep = [], dict(P)
    for m, scale in SETS:
        P.update(m)
        sets.append(([(o["cost"], o["lat"]) for o in build()], P["XL"], P["SL"], scale))
        P.update(keep)
    names = [("BIAS", "tag"), ("FINE", "fine"), ("SB", "st")]
    names = [(k, sorted(set(o[f] for o in ops))) for k, f in names]
    z = [12345]

    def rnd(n):
        z[0] = (z[0] * 1103515245 + 12345) % 2147483648
        return (z[0] >> 8) % n

    best = dict((k, P[k]) for k in ("BIAS", "FINE", "SB", "DG"))
    _place(ops, succ, best)
    score = _spans(ops, sets)
    for _ in range(P["TRIES"]):
        p = dict(BIAS=dict(best["BIAS"]), FINE=dict(best["FINE"]), SB=dict(best["SB"]), DG=[list(r) for r in best["DG"]])
        for _ in range(1 + rnd(2)):
            u = rnd(4)
            if u == 3:
                p["DG"][rnd(ST)][rnd(6)] ^= 1 << rnd(SUB)
            else:
                k, ns = names[u]
                nm = ns[rnd(len(ns))]
                p[k][nm] = p[k].get(nm, 0) + (2 * rnd(2) - 1) * (500, 2000, 5000, 12000)[rnd(4)]
        _place(ops, succ, p)
        s = _spans(ops, sets)
        if s[0] <= score[0]:
            best, score = p, s
    order = _place(ops, succ, best)
    need = set(j for o in ops for j in o["hard"])
    total = {}
    for e in order:
        for i in order[e]:
            o = ops[i]
            o["tok"] = None
            if o["kind"] == "dma":
                o["tok"] = (o["sem"], 16)
                total[o["sem"]] = 16
            elif o["kind"] != "send" and i in need:
                total["s_" + e] = total.get("s_" + e, 0) + 1
                o["tok"] = ("s_" + e, total["s_" + e])
    for o in ops:
        if o["kind"] == "recv":
            o["tok"] = (o["sem"], -1)
            o["know"] = {}
    known = dict((e, {}) for e in order)
    seq = sorted([o for o in ops if o["eng"]], key=lambda x: (x["start"], x["i"]))
    for o in seq:
        kn = known[o["eng"]]
        waits = {}
        for j in sorted(o["hard"], key=lambda j: -ops[j]["start"]):
            s, v = ops[j]["tok"]
            if s in kn and kn[s] >= v:
                continue
            waits[s] = max(waits.get(s, v), v)
            kn[s] = v
            for s2, v2 in ops[j]["know"].items():
                if s2 not in kn or kn[s2] < v2:
                    kn[s2] = v2
        o["waits"] = sorted(waits.items())
        o["know"] = dict(kn)
    return seq, order, total, ops, score


_CACHE = []


def rank_program(g, core, T, topo):
    rank = T.rank_of(core)
    if rank is None:
        return
    if not _CACHE:
        _CACHE.append(schedule())
    seq, order, total = _CACHE[0][:3]
    n = len(T.cores)
    dst = T.cores[(rank + HOP) % n]
    src = T.cores[(rank - HOP) % n]

    def lanes(a, b):
        return topo.engines(a, b)[:8]

    mask = sum(1 << e for e in lanes(core, dst))
    n_in = len(lanes(src, core))
    rid, pid, _ = topo.addr(dst)
    Q = dict(dve=g.vector, act=g.scalar, pe=g.tensor, pool=g, sp=g.sync)
    sent = 0
    for o in seq:
        e, k = o["eng"], o["kind"]
        q = Q[e]
        for s, v in o["waits"]:
            q.wait_ge(T.sem[s], n_in if v < 0 else v)
        if k == "send":
            su, lu, arr = o["args"]
            g.remote_dma(T[lu][:, :], T[su][:, :], T.sem[arr], T.sem.sent, pid, rid, mask)
            sent += len(lanes(core, dst))
            continue
        if k == "dma":
            out, in_ = o["args"](T)
            q.dma_start(out, in_).then_inc(T.sem[o["sem"]], 16)
            continue
        a = [_ap(T, x) for x in o["args"]]
        if k == "cp":
            ins = q.tensor_copy(a[0], a[1]) if e == "dve" else q.activation(a[0], a[1], AF.Copy)
        elif k == "ts":
            ins = q.tensor_scalar(*a[:5]) if a[5] is None else q.tensor_scalar(*a)
        elif k == "tt":
            ins = q.tensor_tensor(*a)
        elif k == "scan":
            ins = q.tensor_tensor_scan(*a)
        elif k == "ms":
            ins = q.memset(*a)
        elif k == "act":
            ins = q.activation(a[0], a[1], a[2], bias=a[3], scale=a[4])
        elif k == "mm":
            ins = q.matmul(*a)
        elif BUF[o["args"][0][0]][2] == I:
            ins = g.iota(*a)
        else:
            ins = g.iota(*a, allow_small_or_imprecise_dtypes=True)
        if o["tok"] is not None:
            ins.then_inc(T.sem[o["tok"][0]], 1)
    for s in sorted(total):
        g.wait_ge(T.sem[s], total[s])
    for s in ARRS:
        g.wait_ge(T.sem[s], n_in)
    g.wait_ge(T.sem.sent, sent)
